import numpy as np, ml_dtypes
CORES = [2,3,6,7,58,59,62,63,114,115,118,119]
N = 12
import mx_ref
BF = ml_dtypes.bfloat16
def entries(a):
    return np.ascontiguousarray(a.T).reshape(-1)
def table(e):
    return np.ascontiguousarray(np.reshape(e, (-1, 16)).T).astype(np.int32)
def cols(t, e):
    v = np.concatenate([t.reshape(128, -1, 4), np.zeros((128, 1, 4), BF)], axis=1)
    return np.ascontiguousarray(v[:, e]).reshape(128, -1)
def f(rng, *shape):
    return mx_ref.flush((rng.standard_normal(shape, dtype=np.float32) * np.exp2(rng.integers(-2, 3, shape[:-1] + (1,)))).astype(BF))
def wide(rng, *shape, cols=0):
    v = rng.standard_normal(shape, dtype=np.float32) * np.exp2(rng.integers(-12, 13, shape)).astype(np.float32)
    if cols: v *= np.repeat(np.exp2(rng.integers(-cols, cols + 1, shape[:-2] + (1, shape[-1] // 4))) * (rng.random(shape[:-2] + (1, shape[-1] // 4)) > 0.0625), 4, axis=-1).astype(np.float32)
    return mx_ref.flush(v.astype(BF))
T, S, CAPP = 512, 256, 32
def lists(rng, most=None, own=False, share=False, edge=False):
    o, c, m = [], [], []
    for r in range(N):
        n = np.zeros(N, int)
        if own: n[r] = CAPP
        if most is not None:
            for q in rng.permutation(N)[:most]: n[q] = CAPP
            n = np.minimum(n, np.maximum(0, S - (np.cumsum(n) - n)))
        while n.sum() < S:
            q = rng.integers(0, N)
            if n[q] < CAPP: n[q] += 1
        slots = np.full(N * CAPP, -1); used = []
        for q in range(N):
            k = q * CAPP + rng.permutation(CAPP)[:n[q]]; used += list(k)
            slots[k] = rng.integers(0, T) if share else rng.choice([0, T - 1], n[q]) if edge else rng.integers(0, T, n[q])
        o.append(table(rng.choice([0, T - 1], S) if edge else rng.integers(0, T, S))); c.append(table(slots)); m.append(table(rng.permutation(used)))
    return {"own": np.stack(o), "want": np.stack(c), "slot": np.stack(m)}
def setup_inputs(rng):
    return {"x": f(rng, N, 128, 4 * T), "w": f(rng, N, 128, 512), **lists(rng)}
def setup_inputs_edge(rng):
    return {**setup_inputs(rng), **lists(rng, edge=True)}
def setup_inputs_full(rng):
    return {**setup_inputs(rng), **lists(rng, most=S // CAPP)}
def setup_inputs_self(rng):
    return {**setup_inputs(rng), **lists(rng, own=True)}
def setup_inputs_share(rng):
    return {**setup_inputs(rng), **lists(rng, share=True)}
def setup_inputs_spread(rng):
    d = setup_inputs(rng); d["x"] = wide(rng, N, 128, 4 * T, cols=8); return d
def check_inputs(d):
    b = []
    for r in range(N):
        o, c, m = entries(d["own"][r]), entries(d["want"][r]), entries(d["slot"][r])
        if o.min() < 0 or o.max() >= T: b.append("own")
        if c.min() < -1 or c.max() >= T: b.append("want")
        if m.min() < 0 or m.max() >= N * CAPP or len(set(m.tolist())) != S or (c[m] < 0).any() or (c >= 0).sum() != S: b.append("slot")
    return b
def decode(q):
    out = np.zeros(q[0].shape, np.float32)
    for b in range(4):
        e = np.zeros((128, 128, 4), np.float32); e[np.arange(128), np.arange(128), b] = 1
        out[:, b::4] = mx_ref.matmul(mx_ref.quantize(e.reshape(128, 512).astype(BF)), q)
    return out
def reference(x, w, own, want, slot):
    M = []
    for r in range(N):
        c = entries(want[r])
        arrived = np.concatenate([decode(mx_ref.quantize(cols(x[q], c[q * CAPP:(q + 1) * CAPP]))) for q in range(N)], axis=1)
        far = arrived.reshape(128, -1, 4)[:, entries(slot[r])].reshape(128, -1)
        M.append(mx_ref.quantize(((cols(x[r], entries(own[r])).astype(np.float32) + far) * np.float32(0.5)).astype(BF)))
    y = np.zeros((N, 128, 3 * S), np.float32)
    for r in range(N):
        for i in range(3): y[r][:, S * i:S * i + S] = mx_ref.matmul(mx_ref.quantize(w[r]), M[(r - 1 + i) % N])
    return {"y": y}

@@ -1,0 +1,259 @@
+import numpy as np
+from concourse.bass import DstId, RemoteDMATransfer
+from concourse.mybir import dt, AluOpType, ActivationFunctionType
+
+F8, U8, F32, BF, I32, U16 = "float8_e4m3fn_x4", "uint8", "float32", "bfloat16", "int32", "uint16"
+SCRATCH = {
+    "lsend": ("dram", [192, 2], I32),
+    "lland": ("dram", [12, 128, 2], I32),
+    "xs": ("sbuf", [128, 2048], BF),
+    "ws": ("sbuf", [128, 512], BF),
+    "wc": ("sbuf", [128, 128], F8), "wp": ("sbuf", [128, 128], U8),
+    "ones": ("sbuf", [128, 516], BF), "band": ("sbuf", [128, 516], BF),
+    "ec": ("sbuf", [128, 512], F8), "ep": ("sbuf", [128, 512], U8),
+    "raw": ("sbuf", [16, 32], I32),
+    "i1": ("sbuf", [16, 16], I32), "i2": ("sbuf", [16, 16], I32), "i3": ("sbuf", [16, 16], I32),
+    "i4": ("sbuf", [16, 16], I32), "i5": ("sbuf", [16, 16], I32), "i6": ("sbuf", [16, 16], I32), "i7": ("sbuf", [16, 16], I32),
+    "oo": ("sbuf", [128, 32], U16),
+    "lf": ("sbuf", [128, 32], I32), "ff": ("sbuf", [128, 64], F32), "tf": ("sbuf", [128, 64], F32), "of": ("sbuf", [128, 16], U16),
+    "ln": ("sbuf", [128, 32], I32), "fn": ("sbuf", [128, 64], F32), "tn": ("sbuf", [128, 64], F32), "on": ("sbuf", [128, 8], U16),
+    "h": ("sbuf", [128, 1536], BF),
+    "cq": ("sbuf", [128, 384], F8), "sq": ("sbuf", [128, 384], U8),
+    "cf": ("sbuf", [128, 384], F8), "sf": ("sbuf", [128, 384], U8),
+    "f": ("sbuf", [128, 1536], F32),
+    "ow": ("sbuf", [128, 1024], BF),
+    "m": ("sbuf", [128, 1024], BF),
+    "mc": ("sbuf", [128, 256], F8), "mp": ("sbuf", [128, 256], U8),
+    "lc": ("sbuf", [128, 256], F8), "lp": ("sbuf", [128, 256], U8),
+    "rc": ("sbuf", [128, 256], F8), "rp": ("sbuf", [128, 256], U8),
+    "ys": ("sbuf", [128, 768], F32),
+    "pa": ("psum", [128, 2048], F32), "pb": ("psum", [128, 2048], F32),
+}
+SEMAPHORES = ["wnt", "self", "xld", "wld", "old", "rep", "lfl", "lnl", "slf", "yst",
+              "lfa", "lna", "sent", "c0", "c1", "c2", "nl", "nr",
+              "ones", "zf", "zn", "band", "eq", "wq", "d1", "d2", "d3", "d4", "d5", "ofs",
+              "fc", "ft", "fo", "nc", "nt", "no", "g0", "g1", "g2", "q0", "q1", "q2", "ow",
+              "p1", "p2", "ga", "mq", "mo", "ml", "mr", "co", "cl", "cr"] \
+             + ["m%d_%d" % (k, b) for k in range(3) for b in range(4)] + ["k%d" % b for b in range(4)]
+CAPP, S, XC = 32, 256, 512
+
+
+def rank_program(g, core, T, topo):
+    rank = T.rank_of(core)
+    if rank is None:
+        return
+    cores, n = list(T.cores), len(T.cores)
+    chips = []
+    for c in cores:
+        if topo.chip(c) not in chips:
+            chips.append(topo.chip(c))
+    nc = len(chips)
+    members = [[c for c in cores if topo.chip(c) == ch] for ch in chips]
+    me = chips.index(topo.chip(core))
+    loc = members[me].index(core)
+    per = len(members[me])
+    order = [members[(me + 1) % nc], members[(me + 2) % nc], members[me]]
+    V, A, Y, P = g.vector, g.scalar, g.sync, g.tensor
+    mx, mult, add, sub = AluOpType.max, AluOpType.mult, AluOpType.add, AluOpType.subtract
+    tot, sem = {}, T.sem
+
+    def up(call, name, k=1):
+        call.then_inc(sem[name], k)
+        tot[name] = tot.get(name, 0) + k
+
+    def wait(queue, *names):
+        for s in names:
+            queue.wait_ge(sem[s], tot[s])
+
+    def bits(engines):
+        return sum(1 << e for e in engines)
+
+    def dst(c):
+        rid, pid, _ = topo.addr(c)
+        return DstId(rid=rid, pnc=pid)
+
+    def send(transfers):
+        g.remote_dma_fused([RemoteDMATransfer(dst_ids=[dst(c) for c in cs], dma_engine_mask=bits(en), remote_sem=sem[rs], srcs=[src], dsts=list(ds))
+                            for src, ds, cs, en, rs in transfers], local_sem=sem["sent"])
+        tot["sent"] = tot.get("sent", 0) + sum(len(t[3]) for t in transfers)
+
+    off_e = list(topo.engines(core, order[0][0]))
+    all_e = list(topo.engines(core, [c for c in members[me] if c != core][0]))
+    in_e = [e for e in all_e if e not in off_e]
+
+    for k in range(n):
+        q = cores.index(order[k // per][k % per])
+        up((Y if k % 2 == 0 else A).dma_start(T.lsend[16 * k:16 * k + 16, :], T.want[:, 2 * q:2 * q + 2]), "wnt", 16)
+    up(Y.dma_start(T.raw[:, 0:16], T.own[:]), "old", 16)
+    up(A.dma_start(T.raw[:, 16:32], T.slot[:]), "old", 16)
+    up(Y.dma_start(T.xs[:], T.x[:]), "xld", 16)
+    up(A.dma_start(T.ws[:], T.w[:]), "wld", 16)
+    up(Y.dma_start(T.lland[2 * per + loc, 64 + 16 * loc:80 + 16 * loc, :], T.want[:, 2 * rank:2 * rank + 2]), "self", 16)
+
+    up(V.memset(T.ones[:], 1.0), "ones")
+    up(V.memset(T.lf[:], 0), "zf")
+    up(V.memset(T.ln[:], 0), "zn")
+    wait(g, "ones")
+    up(g.affine_select(T.band[:], T.ones[:], [[1, 516]], AluOpType.is_equal, 0.0, -3, -4), "band")
+
+    wait(g, "wnt")
+    one, two = T.lsend[0:128, :], T.lsend[64:192, :]
+    send([(one, [T.lland[per + loc]] * per, order[0], off_e[0:1], "lfa"),
+          (two, [T.lland[loc]] * per, order[1], off_e[1:2], "lfa")])
+    peers = [c for c in members[me] if c != core]
+    send([(two, [T.lland[2 * per + loc]] * len(peers), peers, all_e, "lna")])
+    tot["lfa"] = 2 * per
+    tot["lna"] = len(peers) * len(all_e)
+
+    wait(V, "band")
+    for b in range(4):
+        up(V.quantize_mx(T.ec[:, 128 * b:128 * b + 128], T.ep[:, 128 * b:128 * b + 128], T.band[:, 3 - b:515 - b]), "eq")
+    wait(V, "old")
+    own, slot = T.raw[:, 0:16], T.raw[:, 16:32]
+    up(V.tensor_scalar(T.oo[0:16, 0:16], own, 4, None, mult), "ofs")
+    up(V.tensor_scalar(T.i1[:], slot, 15, None, AluOpType.bitwise_and), "d1")
+    up(V.tensor_scalar(T.i2[:], slot, 4, 1, AluOpType.logical_shift_right, AluOpType.bitwise_and), "d1")
+    wait(V, "d1")
+    up(V.tensor_tensor(T.i3[:], slot, T.i1[:], add), "d2")
+    up(V.tensor_scalar(T.i4[:], T.i2[:], -15, None, mult), "d2")
+    wait(V, "d2")
+    up(V.tensor_tensor(T.i5[:], T.i3[:], T.i4[:], add), "d3")
+    wait(V, "d3")
+    turn = CAPP * per * ((me + 1) % nc)
+    up(V.tensor_scalar(T.i6[:], T.i5[:], turn, CAPP * n, AluOpType.is_lt, mult), "d4")
+    wait(V, "d4")
+    up(V.tensor_tensor(T.i7[:], T.i5[:], T.i6[:], add), "d5")
+    wait(V, "d5")
+    up(V.tensor_scalar(T.oo[0:16, 16:32], T.i7[:], turn, None, sub), "ofs")
+    wait(V, "wld")
+    up(V.quantize_mx(T.wc[:], T.wp[:], T.ws[:]), "wq")
+
+    wait(Y, "ofs")
+    for k in range(1, 8):
+        up(Y.dma_start(T.oo[16 * k:16 * k + 16, :], T.oo[0:16, :]), "rep", 16)
+
+    for q, blocks in ((A, (0, 1)), (Y, (2, 3))):
+        wait(q, "zf", "lfa")
+        for a in blocks:
+            up(q.dma_start(T.lf[32 * a:32 * a + 2 * per, :], T.lland[0:2 * per, 16 * loc:16 * loc + 16, :]), "lfl", 16)
+    wait(Y, "zn", "self", "lna")
+    for a in range(4):
+        up(Y.dma_start(T.ln[32 * a:32 * a + per, :], T.lland[2 * per:3 * per, 64 + 16 * loc:80 + 16 * loc, :]), "lnl", 16)
+
+    def lists(raw, wide, turned, off, k, loaded, s1, s2, s3):
+        wait(V, loaded)
+        for j in range(4):
+            up(V.tensor_scalar(wide[:, 16 * j:16 * j + 16], raw[:, 16 * (j // 2):16 * (j // 2) + 16], 0, 4, mx, mult), s1)
+        wait(V, s1)
+        up(V.transpose(turned[:], wide[:]), s2)
+        wait(V, s2)
+        for t in range(2):
+            up(V.tensor_copy(off[:, t:2 * k:2], turned[:, 32 * t:32 * t + k]), s3)
+
+    def gather(k, off, j):
+        for t in range(4):
+            out, win = T.h[:, 512 * k + t:512 * k + 512:4], T.xs[:, t:4 * XC].indirect(off[:, j:j + 8])
+            if t < 2:
+                up(V.tensor_copy(out, win), "g%d" % k)
+            else:
+                up(A.activation(out, win, ActivationFunctionType.Copy), "g%d" % k)
+        wait(V, "g%d" % k)
+        up(V.quantize_mx(T.cq[:, 128 * k:128 * k + 128], T.sq[:, 128 * k:128 * k + 128], T.h[:, 512 * k:512 * k + 512]), "q%d" % k)
+
+    lists(T.lf, T.ff, T.tf, T.of, 2 * per, "lfl", "fc", "ft", "fo")
+    wait(A, "xld", "fo")
+    wait(V, "xld", "fo")
+    for k in range(2):
+        gather(k, T.of, 8 * k)
+    lists(T.ln, T.fn, T.tn, T.on, per, "lnl", "nc", "nt", "no")
+    wait(A, "no")
+    wait(V, "no")
+    gather(2, T.on, 0)
+
+    half = len(in_e) // 2
+    near_e = [in_e[:half], in_e[half:half + half // 2], in_e[half + half // 2:]]
+    w = len(off_e) // per
+    for k in range(3):
+        wait(g, "q%d" % k)
+        to = [(j, c) for j, c in enumerate(order[k]) if c != core]
+        eng = [off_e[w * i:w * i + w] for i in range(per)] if k < 2 else near_e
+        place = CAPP * ((per, 0, 2 * per)[k] + loc)
+        rs = ("c1", "c0", "c2")[k]
+        for codes in (True, False):
+            tr = []
+            for i, (j, c) in enumerate(to):
+                col = 128 * k + CAPP * j
+                if codes:
+                    s, d = T.cq[:, col:col + CAPP].bitcast(dt.uint8), T.cf[:, place:place + CAPP].bitcast(dt.uint8)
+                else:
+                    s, d = T.sq[:, col:col + CAPP], T.sf[:, place:place + CAPP]
+                tr.append((s, [d], [c], eng[i], rs))
+            send(tr)
+    tot["c0"] = tot["c1"] = 2 * per * w
+    tot["c2"] = sum(2 * len(near_e[[p for p in members[me] if p != c].index(core)]) for c in peers)
+    wait(Y, "q2")
+    mine = 2 * per * CAPP + CAPP * loc
+    up(Y.dma_start(T.cf[:, mine:mine + CAPP].bitcast(dt.uint8), T.cq[:, mine:mine + CAPP].bitcast(dt.uint8)), "slf", 16)
+    up(Y.dma_start(T.sf[:, mine:mine + CAPP], T.sq[:, mine:mine + CAPP]), "slf", 16)
+
+    wait(V, "rep")
+    wait(A, "rep")
+    for b in range(4):
+        out, win = T.ow[:, 256 * b:256 * b + 256], T.xs[:, b:4 * XC].indirect(T.oo[:, 0:16])
+        if b < 2:
+            up(V.tensor_scalar(out, win, 0.5, None, mult), "ow")
+        else:
+            up(A.activation(out, win, ActivationFunctionType.Copy, scale=0.5), "ow")
+
+    wait(P, "eq")
+    for k, ps in ((1, T.pa), (2, T.pb), (0, T.pa)):
+        wait(P, "c%d" % k)
+        if k == 2:
+            wait(P, "slf")
+        if k == 0:
+            wait(P, "p1")
+        for b in range(4):
+            up(P.matmul_mx(ps[:, 512 * b:512 * b + 128], T.ec[:, 128 * b:128 * b + 128], T.ep[:, 128 * b:128 * b + 128],
+                           T.cf[:, 128 * k:128 * k + 128], T.sf[:, 128 * k:128 * k + 128], True, True), "m%d_%d" % (k, b))
+        for b in range(4):
+            wait(A, "m%d_%d" % (k, b))
+            up(A.activation(T.f[:, 384 * b + 128 * k:384 * b + 128 * k + 128], ps[:, 512 * b:512 * b + 128],
+                            ActivationFunctionType.Copy, scale=0.5), "p%d" % k if k else "k%d" % b)
+
+    wait(V, "p1", "p2", "ow")
+    for b in range(4):
+        wait(V, "k%d" % b)
+        up(V.tensor_tensor(T.m[:, b:4 * S:4], T.f[:, 384 * b:384 * b + 384].indirect(T.oo[:, 16:32]), T.ow[:, 256 * b:256 * b + 256], add), "ga")
+    wait(V, "ga")
+    up(V.quantize_mx(T.mc[:], T.mp[:], T.m[:]), "mq")
+    left, right = cores[(rank - 1) % n], cores[(rank + 1) % n]
+    if topo.chip(left) != topo.chip(core):
+        el, er = off_e, in_e
+    else:
+        el, er = in_e, off_e
+    wait(g, "mq")
+    send([(T.mc[:].bitcast(dt.uint8), [T.rc[:].bitcast(dt.uint8)], [left], el, "nr"),
+          (T.mc[:].bitcast(dt.uint8), [T.lc[:].bitcast(dt.uint8)], [right], er, "nl")])
+    send([(T.mp[:], [T.rp[:]], [left], el, "nr"), (T.mp[:], [T.lp[:]], [right], er, "nl")])
+    tot["nl"] = tot["nr"] = 2 * len(off_e)
+
+    def product(codes, plane, bank, s, arrived, i, copier, sc, storer):
+        wait(P, *arrived)
+        up(P.matmul_mx(T.pb[:, 512 * bank:512 * bank + S], T.wc[:], T.wp[:], codes[:], plane[:], True, True), s)
+        wait(copier, s)
+        out, src = T.ys[:, S * i:S * i + S], T.pb[:, 512 * bank:512 * bank + S]
+        if copier is A:
+            up(A.activation(out, src, ActivationFunctionType.Copy), sc)
+        else:
+            up(V.tensor_copy(out, src), sc)
+        wait(storer, sc)
+        up(storer.dma_start(T.y[:, S * i:S * i + S], out), "yst", 16)
+
+    product(T.mc, T.mp, 0, "mo", ("wq", "mq", "p2"), 1, V, "co", Y)
+    sides = [(T.lc, T.lp, 1, "ml", ("nl",), 0, V, "cl", Y), (T.rc, T.rp, 2, "mr", ("nr",), 2, A, "cr", A)]
+    if topo.chip(left) != topo.chip(core):
+        sides.reverse()
+    for s in sides:
+        product(*s)
+    wait(Y, "yst")
+    wait(g, "sent")

@@ -4,38 +4,39 @@ from concourse.mybir import dt, AluOpType, ActivationFunctionType
 
 F8, U8, F32, BF, I32, U16 = "float8_e4m3fn_x4", "uint8", "float32", "bfloat16", "int32", "uint16"
 SCRATCH = {
-    "lsend": ("dram", [192, 2], I32),
-    "lland": ("dram", [12, 128, 2], I32),
+    "wl": ("sbuf", [128, 24], I32),
+    "wo": ("sbuf", [128, 24], U16),
+    "lo": ("sbuf", [128, 32], U16),
+    "sl": ("sbuf", [128, 16], I32),
+    "vals": ("sbuf", [128, 256], I32),
+    "hi": ("sbuf", [128, 16], I32), "s16": ("sbuf", [128, 16], I32),
+    "t0": ("sbuf", [128, 32], F32), "t1": ("sbuf", [128, 32], F32), "so": ("sbuf", [128, 16], U16),
+    "win": ("sbuf", [128, 768], F32), "wt": ("sbuf", [128, 768], F32), "inv": ("sbuf", [128, 24], F32),
+    "oo": ("sbuf", [128, 24], U16),
+    "yo": ("sbuf", [128, 16], U16), "yl": ("sbuf", [128, 16], U16), "yr": ("sbuf", [128, 16], U16),
     "xs": ("sbuf", [128, 2048], BF),
     "ws": ("sbuf", [128, 512], BF),
     "wc": ("sbuf", [128, 128], F8), "wp": ("sbuf", [128, 128], U8),
-    "ones": ("sbuf", [128, 516], BF), "band": ("sbuf", [128, 516], BF),
+    "half": ("sbuf", [128, 128], BF), "band": ("sbuf", [128, 516], BF),
     "ec": ("sbuf", [128, 512], F8), "ep": ("sbuf", [128, 512], U8),
-    "raw": ("sbuf", [16, 32], I32),
-    "i1": ("sbuf", [16, 16], I32), "i2": ("sbuf", [16, 16], I32), "i3": ("sbuf", [16, 16], I32),
-    "i4": ("sbuf", [16, 16], I32), "i5": ("sbuf", [16, 16], I32), "i6": ("sbuf", [16, 16], I32), "i7": ("sbuf", [16, 16], I32),
-    "oo": ("sbuf", [128, 32], U16),
-    "lf": ("sbuf", [128, 32], I32), "ff": ("sbuf", [128, 64], F32), "tf": ("sbuf", [128, 64], F32), "of": ("sbuf", [128, 16], U16),
-    "ln": ("sbuf", [128, 32], I32), "fn": ("sbuf", [128, 64], F32), "tn": ("sbuf", [128, 64], F32), "on": ("sbuf", [128, 8], U16),
     "h": ("sbuf", [128, 1536], BF),
-    "cq": ("sbuf", [128, 384], F8), "sq": ("sbuf", [128, 384], U8),
-    "cf": ("sbuf", [128, 384], F8), "sf": ("sbuf", [128, 384], U8),
-    "f": ("sbuf", [128, 1536], F32),
-    "ow": ("sbuf", [128, 1024], BF),
-    "m": ("sbuf", [128, 1024], BF),
-    "mc": ("sbuf", [128, 256], F8), "mp": ("sbuf", [128, 256], U8),
-    "lc": ("sbuf", [128, 256], F8), "lp": ("sbuf", [128, 256], U8),
-    "rc": ("sbuf", [128, 256], F8), "rp": ("sbuf", [128, 256], U8),
+    "cc": ("sbuf", [128, 736], F8), "cp": ("sbuf", [128, 736], U8),
+    "ow": ("sbuf", [128, 1536], BF),
+    "m": ("sbuf", [128, 1536], BF),
+    "mc": ("sbuf", [128, 384], F8), "mp": ("sbuf", [128, 384], U8),
+    "lc": ("sbuf", [128, 384], F8), "lp": ("sbuf", [128, 384], U8),
+    "rc": ("sbuf", [128, 384], F8), "rp": ("sbuf", [128, 384], U8),
+    "zo": ("sbuf", [128, 384], F32), "zl": ("sbuf", [128, 384], F32), "zr": ("sbuf", [128, 384], F32),
     "ys": ("sbuf", [128, 768], F32),
     "pa": ("psum", [128, 2048], F32), "pb": ("psum", [128, 2048], F32),
 }
-SEMAPHORES = ["wnt", "self", "xld", "wld", "old", "rep", "lfl", "lnl", "slf", "yst",
-              "lfa", "lna", "sent", "c0", "c1", "c2", "nl", "nr",
-              "ones", "zf", "zn", "band", "eq", "wq", "d1", "d2", "d3", "d4", "d5", "ofs",
-              "fc", "ft", "fo", "nc", "nt", "no", "g0", "g1", "g2", "q0", "q1", "q2", "ow",
-              "p1", "p2", "ga", "mq", "mo", "ml", "mr", "co", "cl", "cr"] \
-             + ["m%d_%d" % (k, b) for k in range(3) for b in range(4)] + ["k%d" % b for b in range(4)]
-CAPP, S, XC = 32, 256, 512
+SEMAPHORES = ["wnt", "sld", "old", "xld", "wld", "yst", "sent",
+              "lf", "lg", "ln", "sl_l", "sl_r", "c0", "c1", "c2", "el", "er", "fl", "fr",
+              "zb", "zv", "zw", "band", "eq", "wq", "cv", "mine", "yo", "d1", "d2", "d3", "d4", "d5", "d6", "d7", "oo",
+              "g0", "g1", "g2", "q0", "q1", "q2", "ow", "a0", "a1", "a2", "mq0", "mq1", "mq2",
+              "po", "pel", "per", "pfl", "pfr", "ko", "kl", "kr", "jo", "jl", "jr"] \
+             + ["u%d_%d" % (k, b) for k in range(3) for b in range(4)]
+CAPP, S, XC, CH = 32, 256, 512, 128
 
 
 def rank_program(g, core, T, topo):
@@ -52,9 +53,12 @@ def rank_program(g, core, T, topo):
     me = chips.index(topo.chip(core))
     loc = members[me].index(core)
     per = len(members[me])
-    order = [members[(me + 1) % nc], members[(me + 2) % nc], members[me]]
+    nxt, prv = members[(me + 1) % nc], members[(me - 1) % nc]
+    peers = [members[me][(loc + d) % per] for d in range(1, per)]
+    left, right = cores[(rank - 1) % n], cores[(rank + 1) % n]
     V, A, Y, P = g.vector, g.scalar, g.sync, g.tensor
-    mx, mult, add, sub = AluOpType.max, AluOpType.mult, AluOpType.add, AluOpType.subtract
+    mx, mult, add = AluOpType.max, AluOpType.mult, AluOpType.add
+    Copy = ActivationFunctionType.Copy
     tot, sem = {}, T.sem
 
     def up(call, name, k=1):
@@ -65,195 +69,211 @@ def rank_program(g, core, T, topo):
         for s in names:
             queue.wait_ge(sem[s], tot[s])
 
-    def bits(engines):
-        return sum(1 << e for e in engines)
-
     def dst(c):
         rid, pid, _ = topo.addr(c)
         return DstId(rid=rid, pnc=pid)
 
     def send(transfers):
-        g.remote_dma_fused([RemoteDMATransfer(dst_ids=[dst(c) for c in cs], dma_engine_mask=bits(en), remote_sem=sem[rs], srcs=[src], dsts=list(ds))
-                            for src, ds, cs, en, rs in transfers], local_sem=sem["sent"])
+        g.remote_dma_fused([RemoteDMATransfer(dst_ids=[dst(c)], dma_engine_mask=sum(1 << e for e in en), remote_sem=sem[rs], srcs=[s], dsts=[d])
+                            for s, d, c, en, rs in transfers], local_sem=sem["sent"])
         tot["sent"] = tot.get("sent", 0) + sum(len(t[3]) for t in transfers)
 
-    off_e = list(topo.engines(core, order[0][0]))
-    all_e = list(topo.engines(core, [c for c in members[me] if c != core][0]))
-    in_e = [e for e in all_e if e not in off_e]
+    def share(engines, k):
+        w = len(engines) // k
+        return [engines[w * i:w * i + w] for i in range(k)]
 
-    for k in range(n):
-        q = cores.index(order[k // per][k % per])
-        up((Y if k % 2 == 0 else A).dma_start(T.lsend[16 * k:16 * k + 16, :], T.want[:, 2 * q:2 * q + 2]), "wnt", 16)
-    up(Y.dma_start(T.raw[:, 0:16], T.own[:]), "old", 16)
-    up(A.dma_start(T.raw[:, 16:32], T.slot[:]), "old", 16)
+    off_e = list(topo.engines(core, nxt[0]))
+    in_e = [e for e in topo.engines(core, peers[0]) if e not in off_e]
+    near_e = share(in_e, 2)[:1] + share(share(in_e, 2)[1], 2)
+    el, er = (off_e, in_e) if topo.chip(left) != topo.chip(core) else (in_e, off_e)
+
+    up(V.memset(T.vals[:], 0), "zv")
+    up(V.memset(T.half[:], 0.5), "zb")
+    up(V.memset(T.band[:], 0.0), "zb")
+    up(V.memset(T.win[:], 0.0), "zw")
+    for k in range(8):
+        up((Y, A)[k % 2].dma_start(T.wl[16 * k:16 * k + 16, :], T.want[:]), "wnt", 16)
+    for k in range(8):
+        up((Y, A)[k % 2].dma_start(T.sl[16 * k:16 * k + 16, :], T.slot[:]), "sld", 16)
+    wait(Y, "zv")
+    wait(A, "zv")
+    for k in range(8):
+        up((Y, A)[k % 2].dma_start(T.vals[16 * k:16 * k + 1, :], T.own[:]), "old", 16)
     up(Y.dma_start(T.xs[:], T.x[:]), "xld", 16)
-    up(A.dma_start(T.ws[:], T.w[:]), "wld", 16)
-    up(Y.dma_start(T.lland[2 * per + loc, 64 + 16 * loc:80 + 16 * loc, :], T.want[:, 2 * rank:2 * rank + 2]), "self", 16)
 
-    up(V.memset(T.ones[:], 1.0), "ones")
-    up(V.memset(T.lf[:], 0), "zf")
-    up(V.memset(T.ln[:], 0), "zn")
-    wait(g, "ones")
-    up(g.affine_select(T.band[:], T.ones[:], [[1, 516]], AluOpType.is_equal, 0.0, -3, -4), "band")
-
-    wait(g, "wnt")
-    one, two = T.lsend[0:128, :], T.lsend[64:192, :]
-    send([(one, [T.lland[per + loc]] * per, order[0], off_e[0:1], "lfa"),
-          (two, [T.lland[loc]] * per, order[1], off_e[1:2], "lfa")])
-    peers = [c for c in members[me] if c != core]
-    send([(two, [T.lland[2 * per + loc]] * len(peers), peers, all_e, "lna")])
-    tot["lfa"] = 2 * per
-    tot["lna"] = len(peers) * len(all_e)
-
+    wait(g, "zb")
+    up(g.affine_select(T.band[:, 3:515:4], T.half[:], [[1, 128]], AluOpType.is_equal, 0.0, 0, -1), "band")
     wait(V, "band")
     for b in range(4):
         up(V.quantize_mx(T.ec[:, 128 * b:128 * b + 128], T.ep[:, 128 * b:128 * b + 128], T.band[:, 3 - b:515 - b]), "eq")
-    wait(V, "old")
-    own, slot = T.raw[:, 0:16], T.raw[:, 16:32]
-    up(V.tensor_scalar(T.oo[0:16, 0:16], own, 4, None, mult), "ofs")
-    up(V.tensor_scalar(T.i1[:], slot, 15, None, AluOpType.bitwise_and), "d1")
-    up(V.tensor_scalar(T.i2[:], slot, 4, 1, AluOpType.logical_shift_right, AluOpType.bitwise_and), "d1")
+
+    wait(V, "wnt")
+    up(V.tensor_scalar(T.wo[:], T.wl[:], 0, 4, mx, mult), "cv")
+    up(V.tensor_scalar(T.lo[:, 24:26], T.wl[:, 2 * rank:2 * rank + 2], 0, 4, mx, mult), "mine")
+
+    def wanted(c):
+        q = cores.index(c)
+        return T.wo[:, 2 * q:2 * q + 2]
+
+    wait(g, "cv")
+    one = share(off_e, 2 * per)
+    send([(wanted(c), T.lo[:, 2 * loc:2 + 2 * loc], c, one[2 * j], "lf") for j, c in enumerate(prv)])
+    send([(wanted(c), T.lo[:, 8 + 2 * loc:10 + 2 * loc], c, one[2 * j + 1], "lg") for j, c in enumerate(nxt)])
+    send([(wanted(c), T.lo[:, 22 - 2 * j:24 - 2 * j], c, near_e[j], "ln") for j, c in enumerate(peers)])
+    tot["lf"], tot["lg"], tot["ln"] = per, per, len(in_e)
+
+    wait(V, "sld")
+    up(V.tensor_scalar(T.hi[:], T.sl[:], 496, None, AluOpType.bitwise_and), "d1")
+    up(V.tensor_scalar(T.s16[:], T.sl[:], 16, None, add), "d1")
+    up(V.tensor_copy(T.yo[:], T.sl[:]), "yo")
     wait(V, "d1")
-    up(V.tensor_tensor(T.i3[:], slot, T.i1[:], add), "d2")
-    up(V.tensor_scalar(T.i4[:], T.i2[:], -15, None, mult), "d2")
+    up(V.tensor_tensor(T.t0[:, 0:16], T.sl[:], T.hi[:], add), "d2")
+    up(V.tensor_tensor(T.t0[:, 16:32], T.s16[:], T.hi[:], add), "d2")
     wait(V, "d2")
-    up(V.tensor_tensor(T.i5[:], T.i3[:], T.i4[:], add), "d3")
+    up(V.transpose(T.t1[:], T.t0[:]), "d3")
     wait(V, "d3")
-    turn = CAPP * per * ((me + 1) % nc)
-    up(V.tensor_scalar(T.i6[:], T.i5[:], turn, CAPP * n, AluOpType.is_lt, mult), "d4")
-    wait(V, "d4")
-    up(V.tensor_tensor(T.i7[:], T.i5[:], T.i6[:], add), "d5")
+    up(V.tensor_copy(T.so[:], T.t1[:, 0:16]), "d4")
+    wait(V, "d4", "old", "zw")
+    up(V.tensor_copy(T.win[:].indirect(T.so[:]), T.vals[:]), "d5")
     wait(V, "d5")
-    up(V.tensor_scalar(T.oo[0:16, 16:32], T.i7[:], turn, None, sub), "ofs")
-    wait(V, "wld")
-    up(V.quantize_mx(T.wc[:], T.wp[:], T.ws[:]), "wq")
+    up(V.transpose(T.wt[:], T.win[:]), "d6")
+    wait(V, "d6")
+    up(V.tensor_tensor(T.inv[:], T.wt[:, 0:768:32], T.wt[:, 16:768:32], add), "d7")
+    wait(V, "d7")
+    up(V.tensor_scalar(T.oo[:], T.inv[:], 4, None, mult), "oo")
 
-    wait(Y, "ofs")
-    for k in range(1, 8):
-        up(Y.dma_start(T.oo[16 * k:16 * k + 16, :], T.oo[0:16, :]), "rep", 16)
+    wait(g, "yo")
+    send([(T.yo[:], T.yr[:], left, el, "sl_r"), (T.yo[:], T.yl[:], right, er, "sl_l")])
+    tot["sl_l"] = tot["sl_r"] = len(off_e)
+    wait(Y, "xld")
+    up(Y.dma_start(T.ws[:], T.w[:]), "wld", 16)
 
-    for q, blocks in ((A, (0, 1)), (Y, (2, 3))):
-        wait(q, "zf", "lfa")
-        for a in blocks:
-            up(q.dma_start(T.lf[32 * a:32 * a + 2 * per, :], T.lland[0:2 * per, 16 * loc:16 * loc + 16, :]), "lfl", 16)
-    wait(Y, "zn", "self", "lna")
-    for a in range(4):
-        up(Y.dma_start(T.ln[32 * a:32 * a + per, :], T.lland[2 * per:3 * per, 64 + 16 * loc:80 + 16 * loc, :]), "lnl", 16)
-
-    def lists(raw, wide, turned, off, k, loaded, s1, s2, s3):
-        wait(V, loaded)
-        for j in range(4):
-            up(V.tensor_scalar(wide[:, 16 * j:16 * j + 16], raw[:, 16 * (j // 2):16 * (j // 2) + 16], 0, 4, mx, mult), s1)
-        wait(V, s1)
-        up(V.transpose(turned[:], wide[:]), s2)
-        wait(V, s2)
-        for t in range(2):
-            up(V.tensor_copy(off[:, t:2 * k:2], turned[:, 32 * t:32 * t + k]), s3)
-
-    def gather(k, off, j):
+    def gather(k, j):
         for t in range(4):
-            out, win = T.h[:, 512 * k + t:512 * k + 512:4], T.xs[:, t:4 * XC].indirect(off[:, j:j + 8])
+            out, win = T.h[:, 512 * k + t:512 * k + 512:4], T.xs[:, t:4 * XC].indirect(T.lo[:, j:j + 8])
             if t < 2:
                 up(V.tensor_copy(out, win), "g%d" % k)
             else:
-                up(A.activation(out, win, ActivationFunctionType.Copy), "g%d" % k)
+                up(A.activation(out, win, Copy), "g%d" % k)
         wait(V, "g%d" % k)
-        up(V.quantize_mx(T.cq[:, 128 * k:128 * k + 128], T.sq[:, 128 * k:128 * k + 128], T.h[:, 512 * k:512 * k + 512]), "q%d" % k)
+        up(V.quantize_mx(T.cc[:, CH * k:CH * k + CH], T.cp[:, CH * k:CH * k + CH], T.h[:, 512 * k:512 * k + 512]), "q%d" % k)
 
-    lists(T.lf, T.ff, T.tf, T.of, 2 * per, "lfl", "fc", "ft", "fo")
-    wait(A, "xld", "fo")
-    wait(V, "xld", "fo")
-    for k in range(2):
-        gather(k, T.of, 8 * k)
-    lists(T.ln, T.fn, T.tn, T.on, per, "lnl", "nc", "nt", "no")
-    wait(A, "no")
-    wait(V, "no")
-    gather(2, T.on, 0)
+    wait(A, "xld", "lf")
+    wait(V, "xld", "lf")
+    gather(0, 0)
+    wait(A, "lg")
+    wait(V, "lg")
+    gather(1, 8)
+    wait(A, "ln", "mine")
+    wait(V, "ln", "mine")
+    gather(2, 18)
 
-    half = len(in_e) // 2
-    near_e = [in_e[:half], in_e[half:half + half // 2], in_e[half + half // 2:]]
-    w = len(off_e) // per
-    for k in range(3):
-        wait(g, "q%d" % k)
-        to = [(j, c) for j, c in enumerate(order[k]) if c != core]
-        eng = [off_e[w * i:w * i + w] for i in range(per)] if k < 2 else near_e
-        place = CAPP * ((per, 0, 2 * per)[k] + loc)
-        rs = ("c1", "c0", "c2")[k]
-        for codes in (True, False):
-            tr = []
-            for i, (j, c) in enumerate(to):
-                col = 128 * k + CAPP * j
-                if codes:
-                    s, d = T.cq[:, col:col + CAPP].bitcast(dt.uint8), T.cf[:, place:place + CAPP].bitcast(dt.uint8)
-                else:
-                    s, d = T.sq[:, col:col + CAPP], T.sf[:, place:place + CAPP]
-                tr.append((s, [d], [c], eng[i], rs))
-            send(tr)
-    tot["c0"] = tot["c1"] = 2 * per * w
-    tot["c2"] = sum(2 * len(near_e[[p for p in members[me] if p != c].index(core)]) for c in peers)
-    wait(Y, "q2")
-    mine = 2 * per * CAPP + CAPP * loc
-    up(Y.dma_start(T.cf[:, mine:mine + CAPP].bitcast(dt.uint8), T.cq[:, mine:mine + CAPP].bitcast(dt.uint8)), "slf", 16)
-    up(Y.dma_start(T.sf[:, mine:mine + CAPP], T.sq[:, mine:mine + CAPP]), "slf", 16)
+    OWN, LANDP, LANDN = 3 * CH - CAPP, 4 * CH - CAPP, 5 * CH - CAPP
 
-    wait(V, "rep")
-    wait(A, "rep")
+    def cols(codes, src, at, c, en, rs):
+        if codes:
+            return (T.cc[:, src:src + CAPP].bitcast(dt.uint8), T.cc[:, at:at + CAPP].bitcast(dt.uint8), c, en, rs)
+        return (T.cp[:, src:src + CAPP], T.cp[:, at:at + CAPP], c, en, rs)
+
+    def to_next(codes, eng):
+        return [cols(codes, CAPP * j, LANDP + CAPP * loc, c, eng[j], "c0") for j, c in enumerate(nxt)]
+
+    def to_prev(codes, eng):
+        return [cols(codes, CH + CAPP * j, LANDN + CAPP * loc, c, eng[j], "c2") for j, c in enumerate(prv)]
+
+    def to_peers(codes):
+        return [cols(codes, 2 * CH + CAPP * j, OWN + CAPP * (per - 1 - j), c, near_e[j], "c1") for j, c in enumerate(peers)]
+
+    two = share(off_e, per)
+    wait(g, "q0")
+    send(to_next(True, two))
+    wait(g, "q1")
+    send(to_next(False, one[0::2]) + to_prev(False, one[1::2]))
+    wait(g, "q2")
+    send(to_prev(True, two) + to_peers(True))
+    send(to_peers(False))
+    tot["c0"] = tot["c2"] = len(off_e) + per
+    tot["c1"] = 2 * len(in_e)
+
+    wait(V, "oo")
+    wait(A, "oo")
     for b in range(4):
-        out, win = T.ow[:, 256 * b:256 * b + 256], T.xs[:, b:4 * XC].indirect(T.oo[:, 0:16])
+        out, win = T.ow[:, 384 * b:384 * b + 384], T.xs[:, b:4 * XC].indirect(T.oo[:])
         if b < 2:
             up(V.tensor_scalar(out, win, 0.5, None, mult), "ow")
         else:
-            up(A.activation(out, win, ActivationFunctionType.Copy, scale=0.5), "ow")
+            up(A.activation(out, win, Copy, scale=0.5), "ow")
+    wait(V, "wld")
+    up(V.quantize_mx(T.wc[:], T.wp[:], T.ws[:]), "wq")
 
     wait(P, "eq")
-    for k, ps in ((1, T.pa), (2, T.pb), (0, T.pa)):
+    wait(V, "ow")
+    for k, (ps, at, turn) in enumerate(((T.pa, LANDP, 0), (T.pb, OWN, CAPP * loc), (T.pa, LANDN, 0))):
+        chip = (me - 1 + k) % nc
         wait(P, "c%d" % k)
+        if k == 1:
+            wait(P, "q2")
         if k == 2:
-            wait(P, "slf")
-        if k == 0:
-            wait(P, "p1")
+            wait(P, "a0")
         for b in range(4):
-            up(P.matmul_mx(ps[:, 512 * b:512 * b + 128], T.ec[:, 128 * b:128 * b + 128], T.ep[:, 128 * b:128 * b + 128],
-                           T.cf[:, 128 * k:128 * k + 128], T.sf[:, 128 * k:128 * k + 128], True, True), "m%d_%d" % (k, b))
+            up(P.matmul_mx(ps[:, 512 * b:512 * b + CH], T.ec[:, 128 * b:128 * b + 128], T.ep[:, 128 * b:128 * b + 128],
+                           T.cc[:, at:at + CH], T.cp[:, at:at + CH], True, True), "u%d_%d" % (k, b))
         for b in range(4):
-            wait(A, "m%d_%d" % (k, b))
-            up(A.activation(T.f[:, 384 * b + 128 * k:384 * b + 128 * k + 128], ps[:, 512 * b:512 * b + 128],
-                            ActivationFunctionType.Copy, scale=0.5), "p%d" % k if k else "k%d" % b)
+            wait(V, "u%d_%d" % (k, b))
+            for a, z, to in ((0, CH - turn, turn), (CH - turn, CH, 0)):
+                if z > a:
+                    o = 384 * b + CH * chip + to
+                    up(V.tensor_tensor(T.m[:, 512 * k + 4 * to + b:512 * k + 4 * (to + z - a):4], ps[:, 512 * b + a:512 * b + z],
+                                       T.ow[:, o:o + z - a], add), "a%d" % k)
+        wait(V, "a%d" % k)
+        up(V.quantize_mx(T.mc[:, CH * k:CH * k + CH], T.mp[:, CH * k:CH * k + CH], T.m[:, 512 * k:512 * k + 512]), "mq%d" % k)
 
-    wait(V, "p1", "p2", "ow")
-    for b in range(4):
-        wait(V, "k%d" % b)
-        up(V.tensor_tensor(T.m[:, b:4 * S:4], T.f[:, 384 * b:384 * b + 384].indirect(T.oo[:, 16:32]), T.ow[:, 256 * b:256 * b + 256], add), "ga")
-    wait(V, "ga")
-    up(V.quantize_mx(T.mc[:], T.mp[:], T.m[:]), "mq")
-    left, right = cores[(rank - 1) % n], cores[(rank + 1) % n]
-    if topo.chip(left) != topo.chip(core):
-        el, er = off_e, in_e
-    else:
-        el, er = in_e, off_e
-    wait(g, "mq")
-    send([(T.mc[:].bitcast(dt.uint8), [T.rc[:].bitcast(dt.uint8)], [left], el, "nr"),
-          (T.mc[:].bitcast(dt.uint8), [T.lc[:].bitcast(dt.uint8)], [right], er, "nl")])
-    send([(T.mp[:], [T.rp[:]], [left], el, "nr"), (T.mp[:], [T.lp[:]], [right], er, "nl")])
-    tot["nl"] = tot["nr"] = 2 * len(off_e)
+    def part(a, z, sl, sr):
+        send([(T.mc[:, a:z].bitcast(dt.uint8), T.rc[:, a:z].bitcast(dt.uint8), left, el, sr),
+              (T.mc[:, a:z].bitcast(dt.uint8), T.lc[:, a:z].bitcast(dt.uint8), right, er, sl)])
+        send([(T.mp[:, a:z], T.rp[:, a:z], left, el, sr), (T.mp[:, a:z], T.lp[:, a:z], right, er, sl)])
+        tot[sl] = tot[sr] = 2 * len(off_e)
 
-    def product(codes, plane, bank, s, arrived, i, copier, sc, storer):
+    wait(g, "mq0", "mq1")
+    part(0, 2 * CH, "el", "er")
+    wait(g, "mq2")
+    part(2 * CH, 3 * CH, "fl", "fr")
+
+    def copy(q, out, src, s):
+        up(V.tensor_copy(out, src) if q is V else A.activation(out, src, Copy), s)
+
+    def product(c, codes, plane, a, z, ps, at, arrived, s, q, z_out, sk):
         wait(P, *arrived)
-        up(P.matmul_mx(T.pb[:, 512 * bank:512 * bank + S], T.wc[:], T.wp[:], codes[:], plane[:], True, True), s)
-        wait(copier, s)
-        out, src = T.ys[:, S * i:S * i + S], T.pb[:, 512 * bank:512 * bank + S]
-        if copier is A:
-            up(A.activation(out, src, ActivationFunctionType.Copy), sc)
-        else:
-            up(V.tensor_copy(out, src), sc)
-        wait(storer, sc)
-        up(storer.dma_start(T.y[:, S * i:S * i + S], out), "yst", 16)
+        up(P.matmul_mx(ps[:, at:at + z - a], T.wc[:], T.wp[:], codes[:, a:z], plane[:, a:z], True, True), s)
+        wait(q, s)
+        first = (chips.index(topo.chip(c)) - 1) % nc
+        runs = []
+        for k in range(a // CH, z // CH):
+            to = CH * ((first + k) % nc)
+            if runs and runs[-1][1] + runs[-1][2] == to:
+                runs[-1][2] += CH
+            else:
+                runs.append([CH * k - a, to, CH])
+        for frm, to, w in runs:
+            copy(q, z_out[:, to:to + w], ps[:, at + frm:at + frm + w], sk)
 
-    product(T.mc, T.mp, 0, "mo", ("wq", "mq", "p2"), 1, V, "co", Y)
-    sides = [(T.lc, T.lp, 1, "ml", ("nl",), 0, V, "cl", Y), (T.rc, T.rp, 2, "mr", ("nr",), 2, A, "cr", A)]
+    def finish(q, i, z_in, off, needs, s, storer):
+        wait(q, *needs)
+        copy(q, T.ys[:, S * i:S * i + S], z_in[:].indirect(off[:]), s)
+        wait(storer, s)
+        up(storer.dma_start(T.y[:, S * i:S * i + S], T.ys[:, S * i:S * i + S]), "yst", 16)
+
+    product(core, T.mc, T.mp, 0, 3 * CH, T.pb, 0, ("wq", "mq0", "mq1", "mq2"), "po", V, T.zo, "ko")
+    finish(V, 1, T.zo, T.yo, ("ko", "yo"), "jo", Y)
+    product(left, T.lc, T.lp, 0, 2 * CH, T.pb, 512, ("el",), "pel", V, T.zl, "kl")
+    product(right, T.rc, T.rp, 0, 2 * CH, T.pb, 1024, ("er",), "per", A, T.zr, "kr")
+    last = [(left, T.lc, T.lp, 2 * CH, 3 * CH, T.pb, 1536, ("fl",), "pfl", V, T.zl, "kl"),
+            (right, T.rc, T.rp, 2 * CH, 3 * CH, T.pa, 0, ("fr",), "pfr", A, T.zr, "kr")]
     if topo.chip(left) != topo.chip(core):
-        sides.reverse()
-    for s in sides:
+        last.reverse()
+    for s in last:
         product(*s)
+    finish(V, 0, T.zl, T.yl, ("kl", "sl_l"), "jl", Y)
+    finish(A, 2, T.zr, T.yr, ("kr", "sl_r"), "jr", A)
     wait(Y, "yst")
     wait(g, "sent")

@@ -12,7 +12,7 @@ SCRATCH = {
     "hi": ("sbuf", [128, 16], I32), "s16": ("sbuf", [128, 16], I32),
     "t0": ("sbuf", [128, 32], F32), "t1": ("sbuf", [128, 32], F32), "so": ("sbuf", [128, 16], U16),
     "win": ("sbuf", [128, 768], F32), "wt": ("sbuf", [128, 768], F32), "inv": ("sbuf", [128, 24], F32),
-    "oo": ("sbuf", [128, 24], U16),
+    "oo": ("sbuf", [128, 40], U16),
     "yo": ("sbuf", [128, 16], U16), "yl": ("sbuf", [128, 16], U16), "yr": ("sbuf", [128, 16], U16),
     "xs": ("sbuf", [128, 2048], BF),
     "ws": ("sbuf", [128, 512], BF),
@@ -33,8 +33,8 @@ SCRATCH = {
 SEMAPHORES = ["wnt", "sld", "old", "xld", "wld", "yst", "sent",
               "lf", "lg", "ln", "sl_l", "sl_r", "c0", "c1", "c2", "el", "er", "fl", "fr",
               "zb", "zv", "zw", "band", "eq", "wq", "cv", "mine", "yo", "d1", "d2", "d3", "d4", "d5", "d6", "d7", "oo",
-              "g0", "g1", "g2", "q0", "q1", "q2", "ow", "a0", "a1", "a2", "mq0", "mq1", "mq2",
-              "po", "pel", "per", "pfl", "pfr", "ko", "kl", "kr", "jo", "jl", "jr"] \
+              "g0", "g1", "g2", "q0", "q1", "q2", "ow0", "ow1", "ow2", "a0", "a1", "a2", "mq0", "mq1", "mq2",
+              "peo", "po", "pel", "per", "pfl", "pfr", "ko", "kl", "kr", "jo", "jvl", "jvr", "jal", "jar"] \
              + ["u%d_%d" % (k, b) for k in range(3) for b in range(4)]
 CAPP, S, XC, CH = 32, 256, 512, 128
 
@@ -87,10 +87,9 @@ def rank_program(g, core, T, topo):
     near_e = share(in_e, 2)[:1] + share(share(in_e, 2)[1], 2)
     el, er = (off_e, in_e) if topo.chip(left) != topo.chip(core) else (in_e, off_e)
 
-    up(V.memset(T.vals[:], 0), "zv")
     up(V.memset(T.half[:], 0.5), "zb")
     up(V.memset(T.band[:], 0.0), "zb")
-    up(V.memset(T.win[:], 0.0), "zw")
+    up(V.memset(T.vals[:], 0), "zv")
     for k in range(8):
         up((Y, A)[k % 2].dma_start(T.wl[16 * k:16 * k + 16, :], T.want[:]), "wnt", 16)
     for k in range(8):
@@ -103,6 +102,9 @@ def rank_program(g, core, T, topo):
 
     wait(g, "zb")
     up(g.affine_select(T.band[:, 3:515:4], T.half[:], [[1, 128]], AluOpType.is_equal, 0.0, 0, -1), "band")
+    wait(A, "band")
+    for a in (0, 384):
+        up(A.activation(T.win[:, a:a + 384], T.band[:, 0:384], Copy, scale=0.0), "zw")
     wait(V, "band")
     for b in range(4):
         up(V.quantize_mx(T.ec[:, 128 * b:128 * b + 128], T.ep[:, 128 * b:128 * b + 128], T.band[:, 3 - b:515 - b]), "eq")
@@ -118,8 +120,8 @@ def rank_program(g, core, T, topo):
     wait(g, "cv")
     one = share(off_e, 2 * per)
     send([(wanted(c), T.lo[:, 2 * loc:2 + 2 * loc], c, one[2 * j], "lf") for j, c in enumerate(prv)])
-    send([(wanted(c), T.lo[:, 8 + 2 * loc:10 + 2 * loc], c, one[2 * j + 1], "lg") for j, c in enumerate(nxt)])
     send([(wanted(c), T.lo[:, 22 - 2 * j:24 - 2 * j], c, near_e[j], "ln") for j, c in enumerate(peers)])
+    send([(wanted(c), T.lo[:, 8 + 2 * loc:10 + 2 * loc], c, one[2 * j + 1], "lg") for j, c in enumerate(nxt)])
     tot["lf"], tot["lg"], tot["ln"] = per, per, len(in_e)
 
     wait(V, "sld")
@@ -140,7 +142,9 @@ def rank_program(g, core, T, topo):
     wait(V, "d6")
     up(V.tensor_tensor(T.inv[:], T.wt[:, 0:768:32], T.wt[:, 16:768:32], add), "d7")
     wait(V, "d7")
-    up(V.tensor_scalar(T.oo[:], T.inv[:], 4, None, mult), "oo")
+    up(V.tensor_scalar(T.oo[:, 0:24], T.inv[:], 4, None, mult), "oo")
+    for a in (24, 32):
+        up(V.tensor_scalar(T.oo[:, a:a + 8], T.inv[:, 8 * me:8 * me + 8], 4, None, mult), "oo")
 
     wait(g, "yo")
     send([(T.yo[:], T.yr[:], left, el, "sl_r"), (T.yo[:], T.yl[:], right, er, "sl_l")])
@@ -161,12 +165,12 @@ def rank_program(g, core, T, topo):
     wait(A, "xld", "lf")
     wait(V, "xld", "lf")
     gather(0, 0)
-    wait(A, "lg")
-    wait(V, "lg")
-    gather(1, 8)
     wait(A, "ln", "mine")
     wait(V, "ln", "mine")
     gather(2, 18)
+    wait(A, "lg")
+    wait(V, "lg")
+    gather(1, 8)
 
     OWN, LANDP, LANDN = 3 * CH - CAPP, 4 * CH - CAPP, 5 * CH - CAPP
 
@@ -184,32 +188,33 @@ def rank_program(g, core, T, topo):
     def to_peers(codes):
         return [cols(codes, 2 * CH + CAPP * j, OWN + CAPP * (per - 1 - j), c, near_e[j], "c1") for j, c in enumerate(peers)]
 
-    two = share(off_e, per)
     wait(g, "q0")
-    send(to_next(True, two))
-    wait(g, "q1")
-    send(to_next(False, one[0::2]) + to_prev(False, one[1::2]))
+    send(to_next(True, one[0::2]))
+    send(to_next(False, one[1::2]))
     wait(g, "q2")
-    send(to_prev(True, two) + to_peers(True))
+    send(to_peers(True))
     send(to_peers(False))
-    tot["c0"] = tot["c2"] = len(off_e) + per
+    wait(g, "q1")
+    send(to_prev(True, one[1::2]))
+    send(to_prev(False, one[0::2]))
+    tot["c0"] = tot["c2"] = 2 * per
     tot["c1"] = 2 * len(in_e)
 
     wait(V, "oo")
     wait(A, "oo")
-    for b in range(4):
-        out, win = T.ow[:, 384 * b:384 * b + 384], T.xs[:, b:4 * XC].indirect(T.oo[:])
-        if b < 2:
-            up(V.tensor_scalar(out, win, 0.5, None, mult), "ow")
-        else:
-            up(A.activation(out, win, Copy, scale=0.5), "ow")
+    for k, j in enumerate((8 * ((me - 1) % nc), 24 + 2 * loc, 8 * ((me + 1) % nc))):
+        for b in range(4):
+            out, win = T.ow[:, 512 * k + CH * b:512 * k + CH * b + CH], T.xs[:, b:4 * XC].indirect(T.oo[:, j:j + 8])
+            if b < 2 and k < 2:
+                up(V.tensor_scalar(out, win, 0.5, None, mult), "ow%d" % k)
+            else:
+                up(A.activation(out, win, Copy, scale=0.5), "ow%d" % k)
     wait(V, "wld")
     up(V.quantize_mx(T.wc[:], T.wp[:], T.ws[:]), "wq")
 
     wait(P, "eq")
-    wait(V, "ow")
-    for k, (ps, at, turn) in enumerate(((T.pa, LANDP, 0), (T.pb, OWN, CAPP * loc), (T.pa, LANDN, 0))):
-        chip = (me - 1 + k) % nc
+    for k, (ps, at) in enumerate(((T.pa, LANDP), (T.pb, OWN), (T.pa, LANDN))):
+        wait(V, "ow%d" % k)
         wait(P, "c%d" % k)
         if k == 1:
             wait(P, "q2")
@@ -220,11 +225,8 @@ def rank_program(g, core, T, topo):
                            T.cc[:, at:at + CH], T.cp[:, at:at + CH], True, True), "u%d_%d" % (k, b))
         for b in range(4):
             wait(V, "u%d_%d" % (k, b))
-            for a, z, to in ((0, CH - turn, turn), (CH - turn, CH, 0)):
-                if z > a:
-                    o = 384 * b + CH * chip + to
-                    up(V.tensor_tensor(T.m[:, 512 * k + 4 * to + b:512 * k + 4 * (to + z - a):4], ps[:, 512 * b + a:512 * b + z],
-                                       T.ow[:, o:o + z - a], add), "a%d" % k)
+            up(V.tensor_tensor(T.m[:, 512 * k + b:512 * k + 512:4], ps[:, 512 * b:512 * b + CH],
+                               T.ow[:, 512 * k + CH * b:512 * k + CH * b + CH], add), "a%d" % k)
         wait(V, "a%d" % k)
         up(V.quantize_mx(T.mc[:, CH * k:CH * k + CH], T.mp[:, CH * k:CH * k + CH], T.m[:, 512 * k:512 * k + 512]), "mq%d" % k)
 
@@ -232,10 +234,12 @@ def rank_program(g, core, T, topo):
         send([(T.mc[:, a:z].bitcast(dt.uint8), T.rc[:, a:z].bitcast(dt.uint8), left, el, sr),
               (T.mc[:, a:z].bitcast(dt.uint8), T.lc[:, a:z].bitcast(dt.uint8), right, er, sl)])
         send([(T.mp[:, a:z], T.rp[:, a:z], left, el, sr), (T.mp[:, a:z], T.lp[:, a:z], right, er, sl)])
-        tot[sl] = tot[sr] = 2 * len(off_e)
+        tot[sl] = tot[sr] = tot.get(sl, 0) + 2 * len(off_e)
 
-    wait(g, "mq0", "mq1")
-    part(0, 2 * CH, "el", "er")
+    wait(g, "mq0")
+    part(0, CH, "el", "er")
+    wait(g, "mq1")
+    part(CH, 2 * CH, "el", "er")
     wait(g, "mq2")
     part(2 * CH, 3 * CH, "fl", "fr")
 
@@ -246,34 +250,45 @@ def rank_program(g, core, T, topo):
         wait(P, *arrived)
         up(P.matmul_mx(ps[:, at:at + z - a], T.wc[:], T.wp[:], codes[:, a:z], plane[:, a:z], True, True), s)
         wait(q, s)
-        first = (chips.index(topo.chip(c)) - 1) % nc
+        home = chips.index(topo.chip(c))
+        there = members[home].index(c)
         runs = []
-        for k in range(a // CH, z // CH):
-            to = CH * ((first + k) % nc)
+        for j in range(a // CAPP, z // CAPP):
+            k, d = j // per, j % per
+            to = CH * ((home - 1 + k) % nc) + CAPP * ((d + there) % per if k == 1 else d)
             if runs and runs[-1][1] + runs[-1][2] == to:
-                runs[-1][2] += CH
+                runs[-1][2] += CAPP
             else:
-                runs.append([CH * k - a, to, CH])
+                runs.append([CAPP * j - a, to, CAPP])
         for frm, to, w in runs:
             copy(q, z_out[:, to:to + w], ps[:, at + frm:at + frm + w], sk)
 
-    def finish(q, i, z_in, off, needs, s, storer):
+    def finish(q, i, a, z, z_in, off, needs, s):
         wait(q, *needs)
-        copy(q, T.ys[:, S * i:S * i + S], z_in[:].indirect(off[:]), s)
-        wait(storer, s)
-        up(storer.dma_start(T.y[:, S * i:S * i + S], T.ys[:, S * i:S * i + S]), "yst", 16)
+        copy(q, T.ys[:, S * i + a:S * i + z], z_in[:].indirect(off[:, a // 16:z // 16]), s)
 
-    product(core, T.mc, T.mp, 0, 3 * CH, T.pb, 0, ("wq", "mq0", "mq1", "mq2"), "po", V, T.zo, "ko")
-    finish(V, 1, T.zo, T.yo, ("ko", "yo"), "jo", Y)
-    product(left, T.lc, T.lp, 0, 2 * CH, T.pb, 512, ("el",), "pel", V, T.zl, "kl")
-    product(right, T.rc, T.rp, 0, 2 * CH, T.pb, 1024, ("er",), "per", A, T.zr, "kr")
-    last = [(left, T.lc, T.lp, 2 * CH, 3 * CH, T.pb, 1536, ("fl",), "pfl", V, T.zl, "kl"),
-            (right, T.rc, T.rp, 2 * CH, 3 * CH, T.pa, 0, ("fr",), "pfr", A, T.zr, "kr")]
+    def store(q, i, a, z, s):
+        wait(q, s)
+        up(q.dma_start(T.y[:, S * i + a:S * i + z], T.ys[:, S * i + a:S * i + z]), "yst", 16)
+
+    product(core, T.mc, T.mp, 0, 2 * CH, T.pb, 0, ("wq", "mq0", "mq1"), "peo", A, T.zo, "ko")
+    product(core, T.mc, T.mp, 2 * CH, 3 * CH, T.pb, 1536, ("mq2",), "po", V, T.zo, "ko")
+    finish(V, 1, 0, S, T.zo, T.yo, ("ko", "yo"), "jo")
+    store(Y, 1, 0, S, "jo")
+    sides = [(left, T.lc, T.lp, T.zl, T.yl, 0, "l"), (right, T.rc, T.rp, T.zr, T.yr, 2, "r")]
     if topo.chip(left) != topo.chip(core):
-        last.reverse()
-    for s in last:
-        product(*s)
-    finish(V, 0, T.zl, T.yl, ("kl", "sl_l"), "jl", Y)
-    finish(A, 2, T.zr, T.yr, ("kr", "sl_r"), "jr", A)
+        sides.reverse()
+    for j, (c, codes, plane, z_out, off, i, s) in enumerate(sides):
+        product(c, codes, plane, 0, 2 * CH, T.pb, 512 + 512 * j, ("e" + s,), "pe" + s, A, z_out, "k" + s)
+    together = topo.chip(left) == topo.chip(right)
+    for step, j in (((0, 0), (0, 1), (1, 0), (1, 1)) if together else ((0, 0), (1, 0), (0, 1), (1, 1))):
+        c, codes, plane, z_out, off, i, s = sides[j]
+        if step == 0:
+            product(c, codes, plane, 2 * CH, 3 * CH, T.pa, 512 * j, ("f" + s,), "pf" + s, (A, V)[j], z_out, "k" + s)
+        else:
+            finish(V, i, 0, S // 2, z_out, off, ("k" + s, "sl_" + s), "jv" + s)
+            finish(A, i, S // 2, S, z_out, off, ("k" + s, "sl_" + s), "ja" + s)
+            store(Y, i, 0, S // 2, "jv" + s)
+            store((Y, A)[j], i, S // 2, S, "ja" + s)
     wait(Y, "yst")
     wait(g, "sent")

@@ -3,15 +3,18 @@ from concourse.bass import DstId, RemoteDMATransfer
 from concourse.mybir import dt, AluOpType, ActivationFunctionType
 
 F8, U8, F32, BF, I32, U16 = "float8_e4m3fn_x4", "uint8", "float32", "bfloat16", "int32", "uint16"
+COPIES = 2
 SCRATCH = {
     "wl": ("sbuf", [128, 24], I32),
     "wo": ("sbuf", [128, 24], U16),
     "lo": ("sbuf", [128, 32], U16),
     "sl": ("sbuf", [128, 16], I32),
+    "sd": ("dram", [128, 2], I32), "sdl": ("dram", [COPIES, 128, 2], I32), "sdr": ("dram", [COPIES, 128, 2], I32),
+    "nl": ("sbuf", [128, 16], I32), "nr": ("sbuf", [128, 16], I32),
     "vals": ("sbuf", [128, 256], I32),
-    "hi": ("sbuf", [128, 16], I32), "s16": ("sbuf", [128, 16], I32),
-    "t0": ("sbuf", [128, 32], F32), "t1": ("sbuf", [128, 32], F32), "so": ("sbuf", [128, 16], U16),
-    "win": ("sbuf", [128, 768], F32), "wt": ("sbuf", [128, 768], F32), "inv": ("sbuf", [128, 24], F32),
+    "s0": ("sbuf", [16, 16], I32), "hi": ("sbuf", [16, 16], I32), "h2": ("sbuf", [16, 16], I32), "s24": ("sbuf", [16, 16], I32),
+    "t0": ("sbuf", [32, 32], F32), "t1": ("sbuf", [32, 32], F32), "so": ("sbuf", [128, 16], U16), "any": ("sbuf", [128, 16], I32),
+    "win": ("sbuf", [128, 384], F32), "row": ("sbuf", [32, 384], U16),
     "oo": ("sbuf", [128, 40], U16),
     "yo": ("sbuf", [128, 16], U16), "yl": ("sbuf", [128, 16], U16), "yr": ("sbuf", [128, 16], U16),
     "xs": ("sbuf", [128, 2048], BF),
@@ -31,7 +34,7 @@ SCRATCH = {
     "pa": ("psum", [128, 2048], F32), "pb": ("psum", [128, 2048], F32),
 }
 SEMAPHORES = ["wnt", "sld", "old", "xld", "wld", "yst", "sent",
-              "lf", "lg", "ln", "sl_l", "sl_r", "c0", "c1", "c2", "el", "er", "fl", "fr",
+              "lf", "lg", "ln", "sl_l", "sl_r", "sl_n", "sdd", "nld", "any", "zt", "zs", "s0", "ood", "c0", "c1", "c2", "el", "er", "fl", "fr",
               "zb", "zv", "zw", "band", "eq", "wq", "cv", "mine", "yo", "d1", "d2", "d3", "d4", "d5", "d6", "d7", "oo",
               "g0", "g1", "g2", "q0", "q1", "q2", "ow0", "ow1", "ow2", "a0", "a1", "a2", "mq0", "mq1", "mq2",
               "peo", "po", "pel", "per", "pfl", "pfr", "ko", "kl", "kr", "jo", "jvl", "jvr", "jal", "jar"] \
@@ -87,24 +90,29 @@ def rank_program(g, core, T, topo):
     near_e = share(in_e, 2)[:1] + share(share(in_e, 2)[1], 2)
     el, er = (off_e, in_e) if topo.chip(left) != topo.chip(core) else (in_e, off_e)
 
+    up(g.iota(T.any[:], [[16, 16]], 0, 1), "any")
+    up(V.memset(T.vals[:], 0), "zv")
     up(V.memset(T.half[:], 0.5), "zb")
     up(V.memset(T.band[:], 0.0), "zb")
-    up(V.memset(T.vals[:], 0), "zv")
+    up(V.memset(T.t0[:], 0.0), "zt")
+    up(Y.dma_start(T.sd[:], T.slot[:]), "sdd", 16)
     for k in range(8):
-        up((Y, A)[k % 2].dma_start(T.wl[16 * k:16 * k + 16, :], T.want[:]), "wnt", 16)
-    for k in range(8):
-        up((Y, A)[k % 2].dma_start(T.sl[16 * k:16 * k + 16, :], T.slot[:]), "sld", 16)
-    wait(Y, "zv")
-    wait(A, "zv")
-    for k in range(8):
-        up((Y, A)[k % 2].dma_start(T.vals[16 * k:16 * k + 1, :], T.own[:]), "old", 16)
+        up((A, Y)[k % 2].dma_start(T.wl[16 * k:16 * k + 16, :], T.want[:]), "wnt", 16)
+    up(A.dma_start(T.sl[0:16, :], T.slot[:]), "s0", 16)
+    for k, q in enumerate((A, A)):
+        wait(q, "zv")
+        up(q.dma_start(T.vals[16 * k:16 * k + 1, :], T.own[:]), "old", 16)
     up(Y.dma_start(T.xs[:], T.x[:]), "xld", 16)
 
     wait(g, "zb")
     up(g.affine_select(T.band[:, 3:515:4], T.half[:], [[1, 128]], AluOpType.is_equal, 0.0, 0, -1), "band")
     wait(A, "band")
-    for a in (0, 384):
-        up(A.activation(T.win[:, a:a + 384], T.band[:, 0:384], Copy, scale=0.0), "zw")
+    up(A.activation(T.win[:], T.band[:, 0:384], Copy, scale=0.0), "zw")
+    up(A.dma_start(T.ws[:], T.w[:]), "wld", 16)
+    for k in range(1, 8):
+        up((A if k < 5 else Y).dma_start(T.sl[16 * k:16 * k + 16, :], T.slot[:]), "sld", 16)
+    wait(V, "any")
+    up(V.tensor_copy(T.so[:], T.any[:]), "zs")
     wait(V, "band")
     for b in range(4):
         up(V.quantize_mx(T.ec[:, 128 * b:128 * b + 128], T.ep[:, 128 * b:128 * b + 128], T.band[:, 3 - b:515 - b]), "eq")
@@ -117,40 +125,41 @@ def rank_program(g, core, T, topo):
         q = cores.index(c)
         return T.wo[:, 2 * q:2 * q + 2]
 
+    wait(g, "sdd")
+    g.remote_dma_fused([RemoteDMATransfer(dst_ids=[dst(left), dst(right)] * COPIES, dma_engine_mask=sum(1 << e for e in off_e), remote_sem=sem["sl_n"],
+                                          srcs=[T.sd[:]], dsts=[d[k] for k in range(COPIES) for d in (T.sdr, T.sdl)])], local_sem=sem["sent"])
+    tot["sent"], tot["sl_n"] = len(off_e), 2 * COPIES * len(off_e)
     wait(g, "cv")
     one = share(off_e, 2 * per)
-    send([(wanted(c), T.lo[:, 2 * loc:2 + 2 * loc], c, one[2 * j], "lf") for j, c in enumerate(prv)])
+    two = share(off_e, per)
+    send([(wanted(c), T.lo[:, 2 * loc:2 + 2 * loc], c, two[j], "lf") for j, c in enumerate(prv)])
+    send([(wanted(c), T.lo[:, 8 + 2 * loc:10 + 2 * loc], c, two[j], "lg") for j, c in enumerate(nxt)])
     send([(wanted(c), T.lo[:, 22 - 2 * j:24 - 2 * j], c, near_e[j], "ln") for j, c in enumerate(peers)])
-    send([(wanted(c), T.lo[:, 8 + 2 * loc:10 + 2 * loc], c, one[2 * j + 1], "lg") for j, c in enumerate(nxt)])
-    tot["lf"], tot["lg"], tot["ln"] = per, per, len(in_e)
+    tot["lf"], tot["lg"], tot["ln"] = len(off_e), len(off_e), len(in_e)
 
-    wait(V, "sld")
-    up(V.tensor_scalar(T.hi[:], T.sl[:], 496, None, AluOpType.bitwise_and), "d1")
-    up(V.tensor_scalar(T.s16[:], T.sl[:], 16, None, add), "d1")
-    up(V.tensor_copy(T.yo[:], T.sl[:]), "yo")
+    wait(V, "s0")
+    up(V.tensor_scalar(T.hi[:], T.sl[0:16, :], 4, None, AluOpType.logical_shift_right), "d1")
+    up(V.tensor_scalar(T.s24[:], T.sl[0:16, :], 24, None, mult), "d1")
     wait(V, "d1")
-    up(V.tensor_tensor(T.t0[:, 0:16], T.sl[:], T.hi[:], add), "d2")
-    up(V.tensor_tensor(T.t0[:, 16:32], T.s16[:], T.hi[:], add), "d2")
-    wait(V, "d2")
-    up(V.transpose(T.t1[:], T.t0[:]), "d3")
+    up(V.tensor_scalar(T.h2[:], T.hi[:], -383, None, mult), "d2")
+    wait(V, "d2", "zt")
+    for a in (0, 16):
+        up(V.tensor_tensor(T.t0[0:16, a:a + 16], T.s24[:], T.h2[:], add), "d3")
     wait(V, "d3")
-    up(V.tensor_copy(T.so[:], T.t1[:, 0:16]), "d4")
-    wait(V, "d4", "old", "zw")
-    up(V.tensor_copy(T.win[:].indirect(T.so[:]), T.vals[:]), "d5")
-    wait(V, "d5")
-    up(V.transpose(T.wt[:], T.win[:]), "d6")
+    up(V.transpose(T.t1[:], T.t0[:]), "d4")
+    wait(V, "d4", "zs")
+    up(V.tensor_copy(T.so[0:32, :], T.t1[:, 0:16]), "d5")
+    wait(V, "d5", "old", "zw")
+    up(V.tensor_copy(T.win[:].indirect(T.so[:]), T.vals[:]), "d6")
     wait(V, "d6")
-    up(V.tensor_tensor(T.inv[:], T.wt[:, 0:768:32], T.wt[:, 16:768:32], add), "d7")
-    wait(V, "d7")
-    up(V.tensor_scalar(T.oo[:, 0:24], T.inv[:], 4, None, mult), "oo")
-    for a in (24, 32):
-        up(V.tensor_scalar(T.oo[:, a:a + 8], T.inv[:, 8 * me:8 * me + 8], 4, None, mult), "oo")
-
-    wait(g, "yo")
-    send([(T.yo[:], T.yr[:], left, el, "sl_r"), (T.yo[:], T.yl[:], right, er, "sl_l")])
-    tot["sl_l"] = tot["sl_r"] = len(off_e)
-    wait(Y, "xld")
-    up(Y.dma_start(T.ws[:], T.w[:]), "wld", 16)
+    up(V.tensor_scalar(T.row[:], T.win[0:32, :], 4, None, mult), "d7")
+    wait(Y, "d7")
+    for k in range(4):
+        up(Y.dma_start(T.oo[32 * k:32 * k + 32, 0:24], T.row[0:32:16, :]), "ood", 16)
+    wait(Y, "sl_n")
+    for a in range(0, 128, 16 * COPIES):
+        up(Y.dma_start(T.nl[a:a + 16 * COPIES, :], T.sdl[:]), "nld", 16)
+        up(Y.dma_start(T.nr[a:a + 16 * COPIES, :], T.sdr[:]), "nld", 16)
 
     def gather(k, j):
         for t in range(4):
@@ -165,12 +174,12 @@ def rank_program(g, core, T, topo):
     wait(A, "xld", "lf")
     wait(V, "xld", "lf")
     gather(0, 0)
-    wait(A, "ln", "mine")
-    wait(V, "ln", "mine")
-    gather(2, 18)
     wait(A, "lg")
     wait(V, "lg")
     gather(1, 8)
+    wait(A, "ln", "mine")
+    wait(V, "ln", "mine")
+    gather(2, 18)
 
     OWN, LANDP, LANDN = 3 * CH - CAPP, 4 * CH - CAPP, 5 * CH - CAPP
 
@@ -186,23 +195,29 @@ def rank_program(g, core, T, topo):
         return [cols(codes, CH + CAPP * j, LANDN + CAPP * loc, c, eng[j], "c2") for j, c in enumerate(prv)]
 
     def to_peers(codes):
-        return [cols(codes, 2 * CH + CAPP * j, OWN + CAPP * (per - 1 - j), c, near_e[j], "c1") for j, c in enumerate(peers)]
+        eng = near_e if codes else [near_e[1] + near_e[2]] + share(near_e[0], 2)
+        return [cols(codes, 2 * CH + CAPP * j, OWN + CAPP * (per - 1 - j), c, eng[j], "c1") for j, c in enumerate(peers)]
 
     wait(g, "q0")
     send(to_next(True, one[0::2]))
     send(to_next(False, one[1::2]))
-    wait(g, "q2")
-    send(to_peers(True))
-    send(to_peers(False))
     wait(g, "q1")
     send(to_prev(True, one[1::2]))
     send(to_prev(False, one[0::2]))
+    wait(g, "q2")
+    send(to_peers(True))
+    send(to_peers(False))
     tot["c0"] = tot["c2"] = 2 * per
     tot["c1"] = 2 * len(in_e)
 
-    wait(V, "oo")
-    wait(A, "oo")
+    wait(V, "ood")
+    wait(A, "ood")
+    for a in (24, 32):
+        up(V.tensor_copy(T.oo[:, a:a + 8], T.oo[:, 8 * me:8 * me + 8]), "oo")
     for k, j in enumerate((8 * ((me - 1) % nc), 24 + 2 * loc, 8 * ((me + 1) % nc))):
+        if k == 1:
+            wait(V, "oo")
+            wait(A, "oo")
         for b in range(4):
             out, win = T.ow[:, 512 * k + CH * b:512 * k + CH * b + CH], T.xs[:, b:4 * XC].indirect(T.oo[:, j:j + 8])
             if b < 2 and k < 2:
@@ -230,18 +245,22 @@ def rank_program(g, core, T, topo):
         wait(V, "a%d" % k)
         up(V.quantize_mx(T.mc[:, CH * k:CH * k + CH], T.mp[:, CH * k:CH * k + CH], T.m[:, 512 * k:512 * k + 512]), "mq%d" % k)
 
-    def part(a, z, sl, sr):
-        send([(T.mc[:, a:z].bitcast(dt.uint8), T.rc[:, a:z].bitcast(dt.uint8), left, el, sr),
-              (T.mc[:, a:z].bitcast(dt.uint8), T.lc[:, a:z].bitcast(dt.uint8), right, er, sl)])
-        send([(T.mp[:, a:z], T.rp[:, a:z], left, el, sr), (T.mp[:, a:z], T.lp[:, a:z], right, er, sl)])
-        tot[sl] = tot[sr] = tot.get(sl, 0) + 2 * len(off_e)
+    def part(codes, a, z, sl, sr):
+        if codes:
+            send([(T.mc[:, a:z].bitcast(dt.uint8), T.rc[:, a:z].bitcast(dt.uint8), left, el, sr),
+                  (T.mc[:, a:z].bitcast(dt.uint8), T.lc[:, a:z].bitcast(dt.uint8), right, er, sl)])
+        else:
+            send([(T.mp[:, a:z], T.rp[:, a:z], left, el, sr), (T.mp[:, a:z], T.lp[:, a:z], right, er, sl)])
+        tot[sl] = tot[sr] = tot.get(sl, 0) + len(off_e)
 
     wait(g, "mq0")
-    part(0, CH, "el", "er")
+    part(True, 0, CH, "el", "er")
     wait(g, "mq1")
-    part(CH, 2 * CH, "el", "er")
+    part(True, CH, 2 * CH, "el", "er")
+    part(False, 0, 2 * CH, "el", "er")
     wait(g, "mq2")
-    part(2 * CH, 3 * CH, "fl", "fr")
+    part(True, 2 * CH, 3 * CH, "fl", "fr")
+    part(False, 2 * CH, 3 * CH, "fl", "fr")
 
     def copy(q, out, src, s):
         up(V.tensor_copy(out, src) if q is V else A.activation(out, src, Copy), s)
@@ -271,6 +290,10 @@ def rank_program(g, core, T, topo):
         wait(q, s)
         up(q.dma_start(T.y[:, S * i + a:S * i + z], T.ys[:, S * i + a:S * i + z]), "yst", 16)
 
+    wait(V, "sld", "nld")
+    up(V.tensor_copy(T.yo[:], T.sl[:]), "yo")
+    up(V.tensor_copy(T.yl[:], T.nl[:]), "sl_l")
+    up(V.tensor_copy(T.yr[:], T.nr[:]), "sl_r")
     product(core, T.mc, T.mp, 0, 2 * CH, T.pb, 0, ("wq", "mq0", "mq1"), "peo", A, T.zo, "ko")
     product(core, T.mc, T.mp, 2 * CH, 3 * CH, T.pb, 1536, ("mq2",), "po", V, T.zo, "ko")
     finish(V, 1, 0, S, T.zo, T.yo, ("ko", "yo"), "jo")
@@ -288,7 +311,11 @@ def rank_program(g, core, T, topo):
         else:
             finish(V, i, 0, S // 2, z_out, off, ("k" + s, "sl_" + s), "jv" + s)
             finish(A, i, S // 2, S, z_out, off, ("k" + s, "sl_" + s), "ja" + s)
-            store(Y, i, 0, S // 2, "jv" + s)
-            store((Y, A)[j], i, S // 2, S, "ja" + s)
+            if j == 0:
+                wait(Y, "jv" + s)
+                store(Y, i, 0, S, "ja" + s)
+            else:
+                store(Y, i, 0, S // 2, "jv" + s)
+                store(A, i, S // 2, S, "ja" + s)
     wait(Y, "yst")
     wait(g, "sent")

@@ -3,7 +3,7 @@ from concourse.bass import DstId, RemoteDMATransfer
 from concourse.mybir import dt, AluOpType, ActivationFunctionType
 
 F8, U8, F32, BF, I32, U16 = "float8_e4m3fn_x4", "uint8", "float32", "bfloat16", "int32", "uint16"
-COPIES = 2
+COPIES, TURN = 2, 1
 SCRATCH = {
     "wl": ("sbuf", [128, 24], I32),
     "wo": ("sbuf", [128, 24], U16),
@@ -14,7 +14,7 @@ SCRATCH = {
     "vals": ("sbuf", [128, 256], I32),
     "s0": ("sbuf", [16, 16], I32), "hi": ("sbuf", [16, 16], I32), "h2": ("sbuf", [16, 16], I32), "s24": ("sbuf", [16, 16], I32),
     "t0": ("sbuf", [32, 32], F32), "t1": ("sbuf", [32, 32], F32), "so": ("sbuf", [128, 16], U16), "any": ("sbuf", [128, 16], I32),
-    "win": ("sbuf", [128, 384], F32), "row": ("sbuf", [32, 384], U16),
+    "win": ("sbuf", [128, 384], F32), "inv": ("sbuf", [128, 24], F32),
     "oo": ("sbuf", [128, 40], U16),
     "yo": ("sbuf", [128, 16], U16), "yl": ("sbuf", [128, 16], U16), "yr": ("sbuf", [128, 16], U16),
     "xs": ("sbuf", [128, 2048], BF),
@@ -22,8 +22,8 @@ SCRATCH = {
     "wc": ("sbuf", [128, 128], F8), "wp": ("sbuf", [128, 128], U8),
     "half": ("sbuf", [128, 128], BF), "band": ("sbuf", [128, 516], BF),
     "ec": ("sbuf", [128, 512], F8), "ep": ("sbuf", [128, 512], U8),
-    "h": ("sbuf", [128, 1536], BF),
-    "cc": ("sbuf", [128, 736], F8), "cp": ("sbuf", [128, 736], U8),
+    "h": ("sbuf", [128, 2048], BF),
+    "cc": ("sbuf", [128, 864], F8), "cp": ("sbuf", [128, 864], U8),
     "ow": ("sbuf", [128, 1536], BF),
     "m": ("sbuf", [128, 1536], BF),
     "mc": ("sbuf", [128, 384], F8), "mp": ("sbuf", [128, 384], U8),
@@ -36,10 +36,11 @@ SCRATCH = {
 SEMAPHORES = ["wnt", "sld", "old", "xld", "wld", "yst", "sent",
               "lf", "lg", "ln", "sl_l", "sl_r", "sl_n", "sdd", "nld", "any", "zt", "zs", "s0", "ood", "c0", "c1", "c2", "el", "er", "fl", "fr",
               "zb", "zv", "zw", "band", "eq", "wq", "cv", "mine", "yo", "d1", "d2", "d3", "d4", "d5", "d6", "d7", "oo",
-              "g0", "g1", "g2", "q0", "q1", "q2", "ow0", "ow1", "ow2", "a0", "a1", "a2", "mq0", "mq1", "mq2",
-              "peo", "po", "pel", "per", "pfl", "pfr", "ko", "kl", "kr", "jo", "jvl", "jvr", "jal", "jar"] \
-             + ["u%d_%d" % (k, b) for k in range(3) for b in range(4)]
-CAPP, S, XC, CH = 32, 256, 512, 128
+              "gn0", "gn1", "gm", "gp0", "gp1", "qn0", "qn1", "qm", "qp0", "qp1", "lf0", "lf1", "zh", "c3",
+              "ow0", "ow1", "ow2", "a0", "a1", "a2", "a3", "mq0", "mq1", "mq2",
+              "oog", "oo0", "dl", "dr", "pdl", "pdr", "peo", "po", "pel", "per", "pfl", "pfr", "ko", "kl", "kr", "jo", "jvl", "jvr", "jal", "jar"] \
+             + ["%s%d_%d" % (s, k, b) for s in "uo" for k in range(4) for b in range(4)]
+CAPP, S, XC, CH, RELAY = 32, 256, 512, 128, 64
 
 
 def rank_program(g, core, T, topo):
@@ -56,7 +57,8 @@ def rank_program(g, core, T, topo):
     me = chips.index(topo.chip(core))
     loc = members[me].index(core)
     per = len(members[me])
-    nxt, prv = members[(me + 1) % nc], members[(me - 1) % nc]
+    mine = int(topo.die(core) != topo.die(members[me][0]))
+    nxt, prv = members[(me + TURN) % nc], members[(me - TURN) % nc]
     peers = [members[me][(loc + d) % per] for d in range(1, per)]
     left, right = cores[(rank - 1) % n], cores[(rank + 1) % n]
     V, A, Y, P = g.vector, g.scalar, g.sync, g.tensor
@@ -85,6 +87,10 @@ def rank_program(g, core, T, topo):
         w = len(engines) // k
         return [engines[w * i:w * i + w] for i in range(k)]
 
+    def edge(c):
+        q = cores.index(c)
+        return topo.chip(cores[(q - 1) % n]) != topo.chip(cores[(q + 1) % n])
+
     off_e = list(topo.engines(core, nxt[0]))
     in_e = [e for e in topo.engines(core, peers[0]) if e not in off_e]
     near_e = share(in_e, 2)[:1] + share(share(in_e, 2)[1], 2)
@@ -96,10 +102,10 @@ def rank_program(g, core, T, topo):
     up(V.memset(T.band[:], 0.0), "zb")
     up(V.memset(T.t0[:], 0.0), "zt")
     up(Y.dma_start(T.sd[:], T.slot[:]), "sdd", 16)
+    up(A.dma_start(T.sl[0:16, :], T.slot[:]), "s0", 16)
     for k in range(8):
         up((A, Y)[k % 2].dma_start(T.wl[16 * k:16 * k + 16, :], T.want[:]), "wnt", 16)
-    up(A.dma_start(T.sl[0:16, :], T.slot[:]), "s0", 16)
-    for k, q in enumerate((A, A)):
+    for k, q in enumerate((Y, A)):
         wait(q, "zv")
         up(q.dma_start(T.vals[16 * k:16 * k + 1, :], T.own[:]), "old", 16)
     up(Y.dma_start(T.xs[:], T.x[:]), "xld", 16)
@@ -110,38 +116,41 @@ def rank_program(g, core, T, topo):
     up(A.activation(T.win[:], T.band[:, 0:384], Copy, scale=0.0), "zw")
     up(A.dma_start(T.ws[:], T.w[:]), "wld", 16)
     for k in range(1, 8):
-        up((A if k < 5 else Y).dma_start(T.sl[16 * k:16 * k + 16, :], T.slot[:]), "sld", 16)
+        up((A if k < 3 else Y).dma_start(T.sl[16 * k:16 * k + 16, :], T.slot[:]), "sld", 16)
     wait(V, "any")
     up(V.tensor_copy(T.so[:], T.any[:]), "zs")
     wait(V, "band")
     for b in range(4):
         up(V.quantize_mx(T.ec[:, 128 * b:128 * b + 128], T.ep[:, 128 * b:128 * b + 128], T.band[:, 3 - b:515 - b]), "eq")
 
+    wait(V, "s0")
+    up(V.tensor_scalar(T.hi[:], T.sl[0:16, :], 4, None, AluOpType.logical_shift_right), "d1")
+    up(V.tensor_scalar(T.s24[:], T.sl[0:16, :], 24, None, mult), "d1")
+    wait(V, "d1")
+    up(V.tensor_scalar(T.h2[:], T.hi[:], -383, None, mult), "d2")
+
     wait(V, "wnt")
     up(V.tensor_scalar(T.wo[:], T.wl[:], 0, 4, mx, mult), "cv")
-    up(V.tensor_scalar(T.lo[:, 24:26], T.wl[:, 2 * rank:2 * rank + 2], 0, 4, mx, mult), "mine")
 
     def wanted(c):
         q = cores.index(c)
         return T.wo[:, 2 * q:2 * q + 2]
 
     wait(g, "sdd")
-    g.remote_dma_fused([RemoteDMATransfer(dst_ids=[dst(left), dst(right)] * COPIES, dma_engine_mask=sum(1 << e for e in off_e), remote_sem=sem["sl_n"],
-                                          srcs=[T.sd[:]], dsts=[d[k] for k in range(COPIES) for d in (T.sdr, T.sdl)])], local_sem=sem["sent"])
-    tot["sent"], tot["sl_n"] = len(off_e), 2 * COPIES * len(off_e)
+    g.remote_dma_fused([RemoteDMATransfer(dst_ids=[dst(c)] * COPIES, dma_engine_mask=sum(1 << e for e in en), remote_sem=sem["sl_n"],
+                                          srcs=[T.sd[:]], dsts=[d[k] for k in range(COPIES)])
+                        for (c, d), en in zip(((left, T.sdr), (right, T.sdl)), share(off_e, 2))], local_sem=sem["sent"])
+    tot["sent"], tot["sl_n"] = len(off_e), COPIES * len(off_e)
     wait(g, "cv")
-    one = share(off_e, 2 * per)
     two = share(off_e, per)
-    send([(wanted(c), T.lo[:, 2 * loc:2 + 2 * loc], c, two[j], "lf") for j, c in enumerate(prv)])
-    send([(wanted(c), T.lo[:, 8 + 2 * loc:10 + 2 * loc], c, two[j], "lg") for j, c in enumerate(nxt)])
+    at = 2 * sorted(members[me], key=lambda c: not edge(c)).index(core)
+    send([(wanted(c), T.lo[:, at:at + 2], c, two[j], "lf%d" % (not edge(core))) for j, c in enumerate(prv)])
     send([(wanted(c), T.lo[:, 22 - 2 * j:24 - 2 * j], c, near_e[j], "ln") for j, c in enumerate(peers)])
-    tot["lf"], tot["lg"], tot["ln"] = len(off_e), len(off_e), len(in_e)
+    send([(wanted(c), T.lo[:, 8 + 2 * loc:10 + 2 * loc], c, two[j], "lg") for j, c in enumerate(nxt)])
+    tot["lf0"] = tot["lf1"] = len(off_e) // 2
+    tot["lg"] = len(off_e)
+    tot["ln"] = len(in_e)
 
-    wait(V, "s0")
-    up(V.tensor_scalar(T.hi[:], T.sl[0:16, :], 4, None, AluOpType.logical_shift_right), "d1")
-    up(V.tensor_scalar(T.s24[:], T.sl[0:16, :], 24, None, mult), "d1")
-    wait(V, "d1")
-    up(V.tensor_scalar(T.h2[:], T.hi[:], -383, None, mult), "d2")
     wait(V, "d2", "zt")
     for a in (0, 16):
         up(V.tensor_tensor(T.t0[0:16, a:a + 16], T.s24[:], T.h2[:], add), "d3")
@@ -151,116 +160,127 @@ def rank_program(g, core, T, topo):
     up(V.tensor_copy(T.so[0:32, :], T.t1[:, 0:16]), "d5")
     wait(V, "d5", "old", "zw")
     up(V.tensor_copy(T.win[:].indirect(T.so[:]), T.vals[:]), "d6")
-    wait(V, "d6")
-    up(V.tensor_scalar(T.row[:], T.win[0:32, :], 4, None, mult), "d7")
-    wait(Y, "d7")
+    up(V.tensor_scalar(T.lo[:, 24:26], T.wl[:, 2 * rank:2 * rank + 2], 0, 4, mx, mult), "mine")
+    wait(Y, "d6")
     for k in range(4):
-        up(Y.dma_start(T.oo[32 * k:32 * k + 32, 0:24], T.row[0:32:16, :]), "ood", 16)
+        up(Y.dma_start(T.inv[32 * k:32 * k + 32, :], T.win[0:32:16, :]), "ood", 16)
     wait(Y, "sl_n")
     for a in range(0, 128, 16 * COPIES):
         up(Y.dma_start(T.nl[a:a + 16 * COPIES, :], T.sdl[:]), "nld", 16)
         up(Y.dma_start(T.nr[a:a + 16 * COPIES, :], T.sdr[:]), "nld", 16)
 
-    def gather(k, j):
+    HALF = CH // 2
+    NEXT, PREV, NEAR = 0, 3 * HALF, 5 * HALF
+    OWN, LAND = NEAR + CH - CAPP, NEAR + 2 * CH - CAPP
+
+    def gather(s, at, width, j, view, needs, after=()):
+        wait(A, *needs)
+        wait(V, *needs)
         for t in range(4):
-            out, win = T.h[:, 512 * k + t:512 * k + 512:4], T.xs[:, t:4 * XC].indirect(T.lo[:, j:j + 8])
+            out, win = T.h[:, 4 * at + t:4 * (at + width):4], T.xs[:, t:4 * XC].indirect(T.lo[:, j:j + width // 16])
             if t < 2:
-                up(V.tensor_copy(out, win), "g%d" % k)
+                up(V.tensor_copy(out, win), "g" + s)
             else:
-                up(A.activation(out, win, Copy), "g%d" % k)
-        wait(V, "g%d" % k)
-        up(V.quantize_mx(T.cc[:, CH * k:CH * k + CH], T.cp[:, CH * k:CH * k + CH], T.h[:, 512 * k:512 * k + 512]), "q%d" % k)
-
-    wait(A, "xld", "lf")
-    wait(V, "xld", "lf")
-    gather(0, 0)
-    wait(A, "lg")
-    wait(V, "lg")
-    gather(1, 8)
-    wait(A, "ln", "mine")
-    wait(V, "ln", "mine")
-    gather(2, 18)
-
-    OWN, LANDP, LANDN = 3 * CH - CAPP, 4 * CH - CAPP, 5 * CH - CAPP
+                up(A.activation(out, win, Copy), "g" + s)
+        wait(V, "g" + s, *after)
+        up(V.quantize_mx(T.cc[:, view:view + CH], T.cp[:, view:view + CH], T.h[:, 4 * view:4 * (view + CH)]), "q" + s)
 
     def cols(codes, src, at, c, en, rs):
         if codes:
             return (T.cc[:, src:src + CAPP].bitcast(dt.uint8), T.cc[:, at:at + CAPP].bitcast(dt.uint8), c, en, rs)
         return (T.cp[:, src:src + CAPP], T.cp[:, at:at + CAPP], c, en, rs)
 
-    def to_next(codes, eng):
-        return [cols(codes, CAPP * j, LANDP + CAPP * loc, c, eng[j], "c0") for j, c in enumerate(nxt)]
+    def leave(tile, group, places, rs):
+        for turn in range(2):
+            to = [j for j, c in enumerate(group) if edge(c) != bool(turn)]
+            for codes in (True, False):
+                eng = share(in_e if group is peers else off_e[(turn + codes) % 2::2], len(to))
+                send([cols(codes, tile + CAPP * j, places[j], group[j], en, rs) for j, en in zip(to, eng)])
 
-    def to_prev(codes, eng):
-        return [cols(codes, CH + CAPP * j, LANDN + CAPP * loc, c, eng[j], "c2") for j, c in enumerate(prv)]
+    def landing(j):
+        return (LAND, LAND + CH) if j < per // 2 else (LAND + CH, LAND)
 
-    def to_peers(codes):
-        eng = near_e if codes else [near_e[1] + near_e[2]] + share(near_e[0], 2)
-        return [cols(codes, 2 * CH + CAPP * j, OWN + CAPP * (per - 1 - j), c, eng[j], "c1") for j, c in enumerate(peers)]
+    def pick(q, s, at, width, j, t):
+        out, win = T.h[:, 4 * at + t:4 * (at + width):4], T.xs[:, t:4 * XC].indirect(T.lo[:, j:j + width // 16])
+        up(V.tensor_copy(out, win) if q is V else A.activation(out, win, Copy), "g" + s)
 
-    wait(g, "q0")
-    send(to_next(True, one[0::2]))
-    send(to_next(False, one[1::2]))
-    wait(g, "q1")
-    send(to_prev(True, one[1::2]))
-    send(to_prev(False, one[0::2]))
-    wait(g, "q2")
-    send(to_peers(True))
-    send(to_peers(False))
-    tot["c0"] = tot["c2"] = 2 * per
-    tot["c1"] = 2 * len(in_e)
+    def pack(s, view):
+        wait(V, "g" + s)
+        up(V.quantize_mx(T.cc[:, view:view + CH], T.cp[:, view:view + CH], T.h[:, 4 * view:4 * (view + CH)]), "q" + s)
+
+    gather("n0", NEXT, CH, 0, NEXT, ("xld", "lf0", "lf1"))
+    wait(g, "qn0")
+    for turn in range(2):
+        to = [j for j, c in enumerate(nxt) if edge(c) != bool(turn)]
+        for codes in (True, False):
+            send([cols(codes, NEXT + HALF * turn + CAPP * i, landing(j)[0] + CAPP * loc, nxt[j], en, "c0")
+                  for i, (j, en) in enumerate(zip(to, share(off_e[(turn + codes) % 2::2], 2)))])
+    wait(A, "lg")
+    wait(V, "lg")
+    for q, t in ((V, 0), (A, 1), (A, 2), (A, 3)):
+        pick(q, "p0", PREV, CH, 8, t)
+    wait(A, "ln", "mine")
+    wait(V, "ln", "mine")
+    pick(V, "m", NEAR, CH, 18, 0)
+    pack("p0", PREV)
+    wait(g, "qp0")
+    leave(PREV, prv, [landing(j)[1] + CAPP * loc for j in range(per)], "c2")
+    for q, t in ((V, 1), (A, 2), (A, 3)):
+        pick(q, "m", NEAR, CH, 18, t)
+    pack("m", NEAR)
+    wait(V, "ood")
+    up(V.tensor_scalar(T.oo[:, 0:24], T.inv[:], 4, None, mult), "oo0")
+    wait(g, "qm")
+    leave(NEAR, peers, [OWN + CAPP * (per - 1 - j) for j in range(per - 1)], "c1")
+    tot["c0"], tot["c1"], tot["c2"] = 2 * len(off_e), 4 * len(in_e), 2 * len(off_e)
 
     wait(V, "ood")
-    wait(A, "ood")
-    for a in (24, 32):
-        up(V.tensor_copy(T.oo[:, a:a + 8], T.oo[:, 8 * me:8 * me + 8]), "oo")
-    for k, j in enumerate((8 * ((me - 1) % nc), 24 + 2 * loc, 8 * ((me + 1) % nc))):
-        if k == 1:
-            wait(V, "oo")
-            wait(A, "oo")
-        for b in range(4):
+    def own(k, j, rows):
+        for b in rows:
             out, win = T.ow[:, 512 * k + CH * b:512 * k + CH * b + CH], T.xs[:, b:4 * XC].indirect(T.oo[:, j:j + 8])
-            if b < 2 and k < 2:
-                up(V.tensor_scalar(out, win, 0.5, None, mult), "ow%d" % k)
+            if b < (2, 0, 0)[k]:
+                up(V.tensor_scalar(out, win, 0.5, None, mult), "o%d_%d" % (k, b))
             else:
-                up(A.activation(out, win, Copy, scale=0.5), "ow%d" % k)
+                up(A.activation(out, win, Copy, scale=0.5), "o%d_%d" % (k, b))
+
+    for a in (24, 32):
+        up(V.tensor_scalar(T.oo[:, a:a + 8], T.inv[:, 8 * me:8 * me + 8], 4, None, mult), "oo")
+    wait(V, "oo0")
+    wait(A, "oo0")
+    lists = (8 * ((me - TURN) % nc), 24 + 2 * loc, 8 * ((me + TURN) % nc))
+    own(0, lists[0], range(4))
+    wait(A, "oo")
+    own(1, lists[1], range(4))
+    own(2, lists[2], range(4))
     wait(V, "wld")
     up(V.quantize_mx(T.wc[:], T.wp[:], T.ws[:]), "wq")
 
     wait(P, "eq")
-    for k, (ps, at) in enumerate(((T.pa, LANDP), (T.pb, OWN), (T.pa, LANDN))):
-        wait(V, "ow%d" % k)
-        wait(P, "c%d" % k)
-        if k == 1:
-            wait(P, "q2")
-        if k == 2:
-            wait(P, "a0")
+    steps = ((0, T.pa, landing(loc)[0], 0, 0, CH, ("c0",)), (1, T.pb, OWN, 0, 0, CH, ("c1", "qm")),
+             (2, T.pa, landing(loc)[1], 0, 0, CH, ("c2", "a0")))
+    for j, (k, ps, at, frm, to, w, needs) in enumerate(steps):
+        wait(P, *needs)
         for b in range(4):
             up(P.matmul_mx(ps[:, 512 * b:512 * b + CH], T.ec[:, 128 * b:128 * b + 128], T.ep[:, 128 * b:128 * b + 128],
-                           T.cc[:, at:at + CH], T.cp[:, at:at + CH], True, True), "u%d_%d" % (k, b))
+                           T.cc[:, at:at + CH], T.cp[:, at:at + CH], True, True), "u%d_%d" % (j, b))
         for b in range(4):
-            wait(V, "u%d_%d" % (k, b))
-            up(V.tensor_tensor(T.m[:, 512 * k + b:512 * k + 512:4], ps[:, 512 * b:512 * b + CH],
-                               T.ow[:, 512 * k + CH * b:512 * k + CH * b + CH], add), "a%d" % k)
-        wait(V, "a%d" % k)
+            wait(V, "o%d_%d" % (k, b), "u%d_%d" % (j, b))
+            o = 512 * k + CH * b + to
+            up(V.tensor_tensor(T.m[:, 512 * k + 4 * to + b:512 * k + 4 * (to + w):4], ps[:, 512 * b + frm:512 * b + frm + w],
+                               T.ow[:, o:o + w], add), "a%d" % j)
+        wait(V, "a%d" % j)
         up(V.quantize_mx(T.mc[:, CH * k:CH * k + CH], T.mp[:, CH * k:CH * k + CH], T.m[:, 512 * k:512 * k + 512]), "mq%d" % k)
 
-    def part(codes, a, z, sl, sr):
-        if codes:
-            send([(T.mc[:, a:z].bitcast(dt.uint8), T.rc[:, a:z].bitcast(dt.uint8), left, el, sr),
-                  (T.mc[:, a:z].bitcast(dt.uint8), T.lc[:, a:z].bitcast(dt.uint8), right, er, sl)])
-        else:
-            send([(T.mp[:, a:z], T.rp[:, a:z], left, el, sr), (T.mp[:, a:z], T.lp[:, a:z], right, er, sl)])
-        tot[sl] = tot[sr] = tot.get(sl, 0) + len(off_e)
+    def code(buf, a, z):
+        return buf[:, a:z].bitcast(dt.uint8)
 
-    wait(g, "mq0")
-    part(True, 0, CH, "el", "er")
-    wait(g, "mq1")
-    part(True, CH, 2 * CH, "el", "er")
-    part(False, 0, 2 * CH, "el", "er")
-    wait(g, "mq2")
-    part(True, 2 * CH, 3 * CH, "fl", "fr")
-    part(False, 2 * CH, 3 * CH, "fl", "fr")
+    both = ((left, T.rc, T.rp, el, "r"), (right, T.lc, T.lp, er, "l"))
+    for k, s in enumerate("def"):
+        a, z = CH * k, CH * k + CH
+        wait(g, "mq%d" % k)
+        send([(code(T.mc, a, z), code(codes, a, z), c, en, s + side) for c, codes, plane, en, side in both])
+        send([(T.mp[:, a:z], plane[:, a:z], c, en, s + side) for c, codes, plane, en, side in both])
+        tot[s + "l"] = tot[s + "r"] = 2 * len(off_e)
 
     def copy(q, out, src, s):
         up(V.tensor_copy(out, src) if q is V else A.activation(out, src, Copy), s)
@@ -274,7 +294,7 @@ def rank_program(g, core, T, topo):
         runs = []
         for j in range(a // CAPP, z // CAPP):
             k, d = j // per, j % per
-            to = CH * ((home - 1 + k) % nc) + CAPP * ((d + there) % per if k == 1 else d)
+            to = CH * ((home + TURN * (k - 1)) % nc) + CAPP * ((d + there) % per if k == 1 else d)
             if runs and runs[-1][1] + runs[-1][2] == to:
                 runs[-1][2] += CAPP
             else:
@@ -299,15 +319,14 @@ def rank_program(g, core, T, topo):
     finish(V, 1, 0, S, T.zo, T.yo, ("ko", "yo"), "jo")
     store(Y, 1, 0, S, "jo")
     sides = [(left, T.lc, T.lp, T.zl, T.yl, 0, "l"), (right, T.rc, T.rp, T.zr, T.yr, 2, "r")]
-    if topo.chip(left) != topo.chip(core):
+    if topo.chip(left) != topo.chip(core) or edge(right) and not edge(core):
         sides.reverse()
-    for j, (c, codes, plane, z_out, off, i, s) in enumerate(sides):
-        product(c, codes, plane, 0, 2 * CH, T.pb, 512 + 512 * j, ("e" + s,), "pe" + s, A, z_out, "k" + s)
-    together = topo.chip(left) == topo.chip(right)
-    for step, j in (((0, 0), (0, 1), (1, 0), (1, 1)) if together else ((0, 0), (1, 0), (0, 1), (1, 1))):
+    for k, j in ((0, 0), (0, 1), (1, 0), (1, 1), (2, 0), (3, 0), (2, 1), (3, 1)):
         c, codes, plane, z_out, off, i, s = sides[j]
-        if step == 0:
-            product(c, codes, plane, 2 * CH, 3 * CH, T.pa, 512 * j, ("f" + s,), "pf" + s, (A, V)[j], z_out, "k" + s)
+        if k < 2:
+            product(c, codes, plane, CH * k, CH * k + CH, (T.pb, T.pa)[k], 512 + 512 * j, ("de"[k] + s,), "p" + "de"[k] + s, A, z_out, "k" + s)
+        elif k == 2:
+            product(c, codes, plane, 2 * CH, 3 * CH, T.pa, 1536 * j, ("f" + s,), "pf" + s, (A, V)[j], z_out, "k" + s)
         else:
             finish(V, i, 0, S // 2, z_out, off, ("k" + s, "sl_" + s), "jv" + s)
             finish(A, i, S // 2, S, z_out, off, ("k" + s, "sl_" + s), "ja" + s)

import numpy as np
from concourse.bass import DstId, RemoteDMATransfer
from concourse.mybir import dt, AluOpType, ActivationFunctionType

F8, U8, F32, BF, I32, U16 = "float8_e4m3fn_x4", "uint8", "float32", "bfloat16", "int32", "uint16"
COPIES, TURN = 2, 1
SCRATCH = {
    "wl": ("sbuf", [128, 24], I32),
    "wo": ("sbuf", [128, 24], U16),
    "lo": ("sbuf", [128, 32], U16),
    "sl": ("sbuf", [128, 16], I32),
    "sd": ("dram", [128, 2], I32), "sdl": ("dram", [COPIES, 128, 2], I32), "sdr": ("dram", [COPIES, 128, 2], I32),
    "nl": ("sbuf", [128, 16], I32), "nr": ("sbuf", [128, 16], I32),
    "vals": ("sbuf", [128, 256], I32),
    "s0": ("sbuf", [16, 16], I32), "hi": ("sbuf", [16, 16], I32), "h2": ("sbuf", [16, 16], I32), "s24": ("sbuf", [16, 16], I32),
    "t0": ("sbuf", [32, 32], F32), "t1": ("sbuf", [32, 32], F32), "so": ("sbuf", [128, 16], U16), "any": ("sbuf", [128, 16], I32),
    "win": ("sbuf", [128, 384], F32), "inv": ("sbuf", [128, 24], F32),
    "oo": ("sbuf", [128, 40], U16),
    "yo": ("sbuf", [128, 16], U16), "yl": ("sbuf", [128, 16], U16), "yr": ("sbuf", [128, 16], U16),
    "xs": ("sbuf", [128, 2048], BF),
    "ws": ("sbuf", [128, 512], BF),
    "wc": ("sbuf", [128, 128], F8), "wp": ("sbuf", [128, 128], U8),
    "half": ("sbuf", [128, 128], BF), "band": ("sbuf", [128, 516], BF),
    "ec": ("sbuf", [128, 512], F8), "ep": ("sbuf", [128, 512], U8),
    "h": ("sbuf", [128, 2048], BF),
    "cc": ("sbuf", [128, 864], F8), "cp": ("sbuf", [128, 864], U8),
    "ow": ("sbuf", [128, 1536], BF),
    "m": ("sbuf", [128, 1536], BF),
    "mc": ("sbuf", [128, 384], F8), "mp": ("sbuf", [128, 384], U8),
    "lc": ("sbuf", [128, 384], F8), "lp": ("sbuf", [128, 384], U8),
    "rc": ("sbuf", [128, 384], F8), "rp": ("sbuf", [128, 384], U8),
    "zo": ("sbuf", [128, 384], F32), "zl": ("sbuf", [128, 384], F32), "zr": ("sbuf", [128, 384], F32),
    "ys": ("sbuf", [128, 768], F32),
    "pa": ("psum", [128, 2048], F32), "pb": ("psum", [128, 2048], F32),
}
SEMAPHORES = ["wnt", "sld", "old", "xld", "wld", "yst", "sent",
              "lf", "lg", "ln", "sl_l", "sl_r", "sl_n", "sdd", "nld", "any", "zt", "zs", "s0", "ood", "c0", "c1", "c2", "el", "er", "fl", "fr",
              "zb", "zv", "zw", "band", "eq", "wq", "cv", "mine", "yo", "d1", "d2", "d3", "d4", "d5", "d6", "d7", "oo",
              "gn0", "gn1", "gm", "gp0", "gp1", "qn0", "qn1", "qm", "qp0", "qp1", "lf0", "lf1", "zh", "c3",
              "ow0", "ow1", "ow2", "a0", "a1", "a2", "a3", "mq0", "mq1", "mq2",
              "oog", "oo0", "dl", "dr", "pdl", "pdr", "peo", "po", "pel", "per", "pfl", "pfr", "ko", "kl", "kr", "jo", "jvl", "jvr", "jal", "jar"] \
             + ["%s%d_%d" % (s, k, b) for s in "uo" for k in range(4) for b in range(4)]
CAPP, S, XC, CH, RELAY = 32, 256, 512, 128, 64


def rank_program(g, core, T, topo):
    rank = T.rank_of(core)
    if rank is None:
        return
    cores, n = list(T.cores), len(T.cores)
    chips = []
    for c in cores:
        if topo.chip(c) not in chips:
            chips.append(topo.chip(c))
    nc = len(chips)
    members = [[c for c in cores if topo.chip(c) == ch] for ch in chips]
    me = chips.index(topo.chip(core))
    loc = members[me].index(core)
    per = len(members[me])
    mine = int(topo.die(core) != topo.die(members[me][0]))
    nxt, prv = members[(me + TURN) % nc], members[(me - TURN) % nc]
    peers = [members[me][(loc + d) % per] for d in range(1, per)]
    left, right = cores[(rank - 1) % n], cores[(rank + 1) % n]
    V, A, Y, P = g.vector, g.scalar, g.sync, g.tensor
    mx, mult, add = AluOpType.max, AluOpType.mult, AluOpType.add
    Copy = ActivationFunctionType.Copy
    tot, sem = {}, T.sem

    def up(call, name, k=1):
        call.then_inc(sem[name], k)
        tot[name] = tot.get(name, 0) + k

    def wait(queue, *names):
        for s in names:
            queue.wait_ge(sem[s], tot[s])

    def dst(c):
        rid, pid, _ = topo.addr(c)
        return DstId(rid=rid, pnc=pid)

    def send(transfers):
        g.remote_dma_fused([RemoteDMATransfer(dst_ids=[dst(c)], dma_engine_mask=sum(1 << e for e in en), remote_sem=sem[rs], srcs=[s], dsts=[d])
                            for s, d, c, en, rs in transfers], local_sem=sem["sent"])
        tot["sent"] = tot.get("sent", 0) + sum(len(t[3]) for t in transfers)

    def share(engines, k):
        w = len(engines) // k
        return [engines[w * i:w * i + w] for i in range(k)]

    def edge(c):
        q = cores.index(c)
        return topo.chip(cores[(q - 1) % n]) != topo.chip(cores[(q + 1) % n])

    off_e = list(topo.engines(core, nxt[0]))
    in_e = [e for e in topo.engines(core, peers[0]) if e not in off_e]
    near_e = share(in_e, 2)[:1] + share(share(in_e, 2)[1], 2)
    el, er = (off_e, in_e) if topo.chip(left) != topo.chip(core) else (in_e, off_e)

    up(g.iota(T.any[:], [[16, 16]], 0, 1), "any")
    up(V.memset(T.vals[:], 0), "zv")
    up(V.memset(T.half[:], 0.5), "zb")
    up(V.memset(T.band[:], 0.0), "zb")
    up(V.memset(T.t0[:], 0.0), "zt")
    up(Y.dma_start(T.sd[:], T.slot[:]), "sdd", 16)
    up(A.dma_start(T.sl[0:16, :], T.slot[:]), "s0", 16)
    for k in range(8):
        up((A, Y)[k % 2].dma_start(T.wl[16 * k:16 * k + 16, :], T.want[:]), "wnt", 16)
    for k, q in enumerate((Y, A)):
        wait(q, "zv")
        up(q.dma_start(T.vals[16 * k:16 * k + 1, :], T.own[:]), "old", 16)
    up(Y.dma_start(T.xs[:], T.x[:]), "xld", 16)

    wait(g, "zb")
    up(g.affine_select(T.band[:, 3:515:4], T.half[:], [[1, 128]], AluOpType.is_equal, 0.0, 0, -1), "band")
    wait(A, "band")
    up(A.activation(T.win[:], T.band[:, 0:384], Copy, scale=0.0), "zw")
    up(A.dma_start(T.ws[:], T.w[:]), "wld", 16)
    for k in range(1, 8):
        up((A if k < 3 else Y).dma_start(T.sl[16 * k:16 * k + 16, :], T.slot[:]), "sld", 16)
    wait(V, "any")
    up(V.tensor_copy(T.so[:], T.any[:]), "zs")
    wait(V, "band")
    for b in range(4):
        up(V.quantize_mx(T.ec[:, 128 * b:128 * b + 128], T.ep[:, 128 * b:128 * b + 128], T.band[:, 3 - b:515 - b]), "eq")

    wait(V, "s0")
    up(V.tensor_scalar(T.hi[:], T.sl[0:16, :], 4, None, AluOpType.logical_shift_right), "d1")
    up(V.tensor_scalar(T.s24[:], T.sl[0:16, :], 24, None, mult), "d1")
    wait(V, "d1")
    up(V.tensor_scalar(T.h2[:], T.hi[:], -383, None, mult), "d2")

    wait(V, "wnt")
    up(V.tensor_scalar(T.wo[:], T.wl[:], 0, 4, mx, mult), "cv")

    def wanted(c):
        q = cores.index(c)
        return T.wo[:, 2 * q:2 * q + 2]

    wait(g, "sdd")
    g.remote_dma_fused([RemoteDMATransfer(dst_ids=[dst(c)] * COPIES, dma_engine_mask=sum(1 << e for e in en), remote_sem=sem["sl_n"],
                                          srcs=[T.sd[:]], dsts=[d[k] for k in range(COPIES)])
                        for (c, d), en in zip(((left, T.sdr), (right, T.sdl)), share(off_e, 2))], local_sem=sem["sent"])
    tot["sent"], tot["sl_n"] = len(off_e), COPIES * len(off_e)
    wait(g, "cv")
    two = share(off_e, per)
    at = 2 * sorted(members[me], key=lambda c: not edge(c)).index(core)
    send([(wanted(c), T.lo[:, at:at + 2], c, two[j], "lf%d" % (not edge(core))) for j, c in enumerate(prv)])
    send([(wanted(c), T.lo[:, 22 - 2 * j:24 - 2 * j], c, near_e[j], "ln") for j, c in enumerate(peers)])
    send([(wanted(c), T.lo[:, 8 + 2 * loc:10 + 2 * loc], c, two[j], "lg") for j, c in enumerate(nxt)])
    tot["lf0"] = tot["lf1"] = len(off_e) // 2
    tot["lg"] = len(off_e)
    tot["ln"] = len(in_e)

    wait(V, "d2", "zt")
    for a in (0, 16):
        up(V.tensor_tensor(T.t0[0:16, a:a + 16], T.s24[:], T.h2[:], add), "d3")
    wait(V, "d3")
    up(V.transpose(T.t1[:], T.t0[:]), "d4")
    wait(V, "d4", "zs")
    up(V.tensor_copy(T.so[0:32, :], T.t1[:, 0:16]), "d5")
    wait(V, "d5", "old", "zw")
    up(V.tensor_copy(T.win[:].indirect(T.so[:]), T.vals[:]), "d6")
    up(V.tensor_scalar(T.lo[:, 24:26], T.wl[:, 2 * rank:2 * rank + 2], 0, 4, mx, mult), "mine")
    wait(Y, "d6")
    for k in range(4):
        up(Y.dma_start(T.inv[32 * k:32 * k + 32, :], T.win[0:32:16, :]), "ood", 16)
    wait(Y, "sl_n")
    for a in range(0, 128, 16 * COPIES):
        up(Y.dma_start(T.nl[a:a + 16 * COPIES, :], T.sdl[:]), "nld", 16)
        up(Y.dma_start(T.nr[a:a + 16 * COPIES, :], T.sdr[:]), "nld", 16)

    HALF = CH // 2
    NEXT, PREV, NEAR = 0, 3 * HALF, 5 * HALF
    OWN, LAND = NEAR + CH - CAPP, NEAR + 2 * CH - CAPP

    def gather(s, at, width, j, view, needs, after=()):
        wait(A, *needs)
        wait(V, *needs)
        for t in range(4):
            out, win = T.h[:, 4 * at + t:4 * (at + width):4], T.xs[:, t:4 * XC].indirect(T.lo[:, j:j + width // 16])
            if t < 2:
                up(V.tensor_copy(out, win), "g" + s)
            else:
                up(A.activation(out, win, Copy), "g" + s)
        wait(V, "g" + s, *after)
        up(V.quantize_mx(T.cc[:, view:view + CH], T.cp[:, view:view + CH], T.h[:, 4 * view:4 * (view + CH)]), "q" + s)

    def cols(codes, src, at, c, en, rs):
        if codes:
            return (T.cc[:, src:src + CAPP].bitcast(dt.uint8), T.cc[:, at:at + CAPP].bitcast(dt.uint8), c, en, rs)
        return (T.cp[:, src:src + CAPP], T.cp[:, at:at + CAPP], c, en, rs)

    def leave(tile, group, places, rs):
        for turn in range(2):
            to = [j for j, c in enumerate(group) if edge(c) != bool(turn)]
            for codes in (True, False):
                eng = share(in_e if group is peers else off_e[(turn + codes) % 2::2], len(to))
                send([cols(codes, tile + CAPP * j, places[j], group[j], en, rs) for j, en in zip(to, eng)])

    def landing(j):
        return (LAND, LAND + CH) if j < per // 2 else (LAND + CH, LAND)

    def pick(q, s, at, width, j, t):
        out, win = T.h[:, 4 * at + t:4 * (at + width):4], T.xs[:, t:4 * XC].indirect(T.lo[:, j:j + width // 16])
        up(V.tensor_copy(out, win) if q is V else A.activation(out, win, Copy), "g" + s)

    def pack(s, view):
        wait(V, "g" + s)
        up(V.quantize_mx(T.cc[:, view:view + CH], T.cp[:, view:view + CH], T.h[:, 4 * view:4 * (view + CH)]), "q" + s)

    gather("n0", NEXT, CH, 0, NEXT, ("xld", "lf0", "lf1"))
    wait(g, "qn0")
    for turn in range(2):
        to = [j for j, c in enumerate(nxt) if edge(c) != bool(turn)]
        for codes in (True, False):
            send([cols(codes, NEXT + HALF * turn + CAPP * i, landing(j)[0] + CAPP * loc, nxt[j], en, "c0")
                  for i, (j, en) in enumerate(zip(to, share(off_e[(turn + codes) % 2::2], 2)))])
    wait(A, "lg")
    wait(V, "lg")
    for q, t in ((V, 0), (A, 1), (A, 2), (A, 3)):
        pick(q, "p0", PREV, CH, 8, t)
    wait(A, "ln", "mine")
    wait(V, "ln", "mine")
    pick(V, "m", NEAR, CH, 18, 0)
    pack("p0", PREV)
    wait(g, "qp0")
    leave(PREV, prv, [landing(j)[1] + CAPP * loc for j in range(per)], "c2")
    for q, t in ((V, 1), (A, 2), (A, 3)):
        pick(q, "m", NEAR, CH, 18, t)
    pack("m", NEAR)
    wait(V, "ood")
    up(V.tensor_scalar(T.oo[:, 0:24], T.inv[:], 4, None, mult), "oo0")
    wait(g, "qm")
    leave(NEAR, peers, [OWN + CAPP * (per - 1 - j) for j in range(per - 1)], "c1")
    tot["c0"], tot["c1"], tot["c2"] = 2 * len(off_e), 4 * len(in_e), 2 * len(off_e)

    wait(V, "ood")
    def own(k, j, rows):
        for b in rows:
            out, win = T.ow[:, 512 * k + CH * b:512 * k + CH * b + CH], T.xs[:, b:4 * XC].indirect(T.oo[:, j:j + 8])
            if b < (2, 0, 0)[k]:
                up(V.tensor_scalar(out, win, 0.5, None, mult), "o%d_%d" % (k, b))
            else:
                up(A.activation(out, win, Copy, scale=0.5), "o%d_%d" % (k, b))

    for a in (24, 32):
        up(V.tensor_scalar(T.oo[:, a:a + 8], T.inv[:, 8 * me:8 * me + 8], 4, None, mult), "oo")
    wait(V, "oo0")
    wait(A, "oo0")
    lists = (8 * ((me - TURN) % nc), 24 + 2 * loc, 8 * ((me + TURN) % nc))
    own(0, lists[0], range(4))
    wait(A, "oo")
    own(1, lists[1], range(4))
    own(2, lists[2], range(4))
    wait(V, "wld")
    up(V.quantize_mx(T.wc[:], T.wp[:], T.ws[:]), "wq")

    wait(P, "eq")
    steps = ((0, T.pa, landing(loc)[0], 0, 0, CH, ("c0",)), (1, T.pb, OWN, 0, 0, CH, ("c1", "qm")),
             (2, T.pa, landing(loc)[1], 0, 0, CH, ("c2", "a0")))
    for j, (k, ps, at, frm, to, w, needs) in enumerate(steps):
        wait(P, *needs)
        for b in range(4):
            up(P.matmul_mx(ps[:, 512 * b:512 * b + CH], T.ec[:, 128 * b:128 * b + 128], T.ep[:, 128 * b:128 * b + 128],
                           T.cc[:, at:at + CH], T.cp[:, at:at + CH], True, True), "u%d_%d" % (j, b))
        for b in range(4):
            wait(V, "o%d_%d" % (k, b), "u%d_%d" % (j, b))
            o = 512 * k + CH * b + to
            up(V.tensor_tensor(T.m[:, 512 * k + 4 * to + b:512 * k + 4 * (to + w):4], ps[:, 512 * b + frm:512 * b + frm + w],
                               T.ow[:, o:o + w], add), "a%d" % j)
        wait(V, "a%d" % j)
        up(V.quantize_mx(T.mc[:, CH * k:CH * k + CH], T.mp[:, CH * k:CH * k + CH], T.m[:, 512 * k:512 * k + 512]), "mq%d" % k)

    def code(buf, a, z):
        return buf[:, a:z].bitcast(dt.uint8)

    both = ((left, T.rc, T.rp, el, "r"), (right, T.lc, T.lp, er, "l"))
    for k, s in enumerate("def"):
        a, z = CH * k, CH * k + CH
        wait(g, "mq%d" % k)
        send([(code(T.mc, a, z), code(codes, a, z), c, en, s + side) for c, codes, plane, en, side in both])
        send([(T.mp[:, a:z], plane[:, a:z], c, en, s + side) for c, codes, plane, en, side in both])
        tot[s + "l"] = tot[s + "r"] = 2 * len(off_e)

    def copy(q, out, src, s):
        up(V.tensor_copy(out, src) if q is V else A.activation(out, src, Copy), s)

    def product(c, codes, plane, a, z, ps, at, arrived, s, q, z_out, sk):
        wait(P, *arrived)
        up(P.matmul_mx(ps[:, at:at + z - a], T.wc[:], T.wp[:], codes[:, a:z], plane[:, a:z], True, True), s)
        wait(q, s)
        home = chips.index(topo.chip(c))
        there = members[home].index(c)
        runs = []
        for j in range(a // CAPP, z // CAPP):
            k, d = j // per, j % per
            to = CH * ((home + TURN * (k - 1)) % nc) + CAPP * ((d + there) % per if k == 1 else d)
            if runs and runs[-1][1] + runs[-1][2] == to:
                runs[-1][2] += CAPP
            else:
                runs.append([CAPP * j - a, to, CAPP])
        for frm, to, w in runs:
            copy(q, z_out[:, to:to + w], ps[:, at + frm:at + frm + w], sk)

    def finish(q, i, a, z, z_in, off, needs, s):
        wait(q, *needs)
        copy(q, T.ys[:, S * i + a:S * i + z], z_in[:].indirect(off[:, a // 16:z // 16]), s)

    def store(q, i, a, z, s):
        wait(q, s)
        up(q.dma_start(T.y[:, S * i + a:S * i + z], T.ys[:, S * i + a:S * i + z]), "yst", 16)

    wait(V, "sld", "nld")
    up(V.tensor_copy(T.yo[:], T.sl[:]), "yo")
    up(V.tensor_copy(T.yl[:], T.nl[:]), "sl_l")
    up(V.tensor_copy(T.yr[:], T.nr[:]), "sl_r")
    product(core, T.mc, T.mp, 0, 2 * CH, T.pb, 0, ("wq", "mq0", "mq1"), "peo", A, T.zo, "ko")
    product(core, T.mc, T.mp, 2 * CH, 3 * CH, T.pb, 1536, ("mq2",), "po", V, T.zo, "ko")
    finish(V, 1, 0, S, T.zo, T.yo, ("ko", "yo"), "jo")
    store(Y, 1, 0, S, "jo")
    sides = [(left, T.lc, T.lp, T.zl, T.yl, 0, "l"), (right, T.rc, T.rp, T.zr, T.yr, 2, "r")]
    if topo.chip(left) != topo.chip(core) or edge(right) and not edge(core):
        sides.reverse()
    for k, j in ((0, 0), (0, 1), (1, 0), (1, 1), (2, 0), (3, 0), (2, 1), (3, 1)):
        c, codes, plane, z_out, off, i, s = sides[j]
        if k < 2:
            product(c, codes, plane, CH * k, CH * k + CH, (T.pb, T.pa)[k], 512 + 512 * j, ("de"[k] + s,), "p" + "de"[k] + s, A, z_out, "k" + s)
        elif k == 2:
            product(c, codes, plane, 2 * CH, 3 * CH, T.pa, 1536 * j, ("f" + s,), "pf" + s, (A, V)[j], z_out, "k" + s)
        else:
            finish(V, i, 0, S // 2, z_out, off, ("k" + s, "sl_" + s), "jv" + s)
            finish(A, i, S // 2, S, z_out, off, ("k" + s, "sl_" + s), "ja" + s)
            if j == 0:
                wait(Y, "jv" + s)
                store(Y, i, 0, S, "ja" + s)
            else:
                store(Y, i, 0, S // 2, "jv" + s)
                store(A, i, S // 2, S, "ja" + s)
    wait(Y, "yst")
    wait(g, "sent")
